import numpy as np
import ml_dtypes


def mxq(x, axis, fmt="e4m3"):
    dtype, down = {"e4m3": (ml_dtypes.float8_e4m3fn, 7), "e5m2": (ml_dtypes.float8_e5m2, 14)}[fmt]
    v = np.moveaxis(np.asarray(x, np.float32).astype(ml_dtypes.bfloat16).astype(np.float64), axis, -1)
    blocks = v.reshape(v.shape[:-1] + (-1, 32))
    amax = np.abs(blocks).max(-1, keepdims=True)
    byte = np.maximum(np.where(amax > 0, np.frexp(amax)[1] - 1 + 127, 0) - down, 1)
    scale = np.exp2(byte - 127.0)
    codes = (blocks / scale).astype(np.float32).astype(dtype).astype(np.float64)
    return np.moveaxis((codes * scale).reshape(v.shape), -1, axis)


WIDE = False


def mx_kscale(k):
    if not WIDE:
        return np.ones(k)
    levels = np.array([10, -10, 5, -5, 0])
    if k % 512:
        return np.exp2(np.random.permutation(np.resize(levels, k // 32))).repeat(32)
    a = np.empty((k // 512, 16))
    for p in range(k // 512):
        a[p, :8] = np.random.permutation(np.resize(levels, 8))
        for g in range(8):
            far = levels[np.abs(levels - a[p, g]) >= 10]
            a[p, g + 8] = far[np.random.randint(len(far))]
    return np.exp2(a.ravel()).repeat(32)


def f64(x):
    return np.asarray(x).astype(np.float64)


def striped(idx):
    return np.tile(idx.reshape(-1, 16).T, (8, 1)).astype(np.uint16)


def unstriped(offs):
    return offs[:16].T.reshape(-1).astype(np.int64)


def pack_weight(w):
    k, n = w.shape
    w = f64(np.asarray(w, np.float32).astype(ml_dtypes.bfloat16)).reshape(k // 32, 32, n)
    amax = np.abs(w).max(1)
    byte = np.clip(np.where(amax > 0, np.frexp(amax)[1] - 1 + 127 - 7, 1), 1, 254)
    scaled = (w * np.exp2(127.0 - byte)[:, None, :]).reshape(k, n).astype(np.float32)
    words = np.ascontiguousarray(scaled.reshape(k // 512, 128, 4, n).transpose(0, 1, 3, 2)).astype(ml_dtypes.float8_e4m3fn).view(np.uint8)
    return words, np.ascontiguousarray(byte.astype(np.uint8).reshape(k // 512, 16, n))


def unpack_weight(words, scales):
    g, p, n, _ = words.shape
    vals = np.ascontiguousarray(words).view(ml_dtypes.float8_e4m3fn).astype(np.float64) * np.repeat(np.exp2(scales.astype(np.float64) - 127.0), 8, axis=1)[..., None]
    return vals.transpose(0, 1, 3, 2).reshape(g * 512, n)


def sigmoid(v):
    return 1.0 / (1.0 + np.exp(-np.maximum(v, -700.0)))


K, T, S, V, W = 512, 1024, 512, 512, 2048


def setup_inputs():
    n = np.random.standard_normal
    s = mx_kscale(K)[:, None]
    packed_xT = pack_weight(n((K, T)) * s)
    packed_eT = pack_weight(n((K, W)) / np.sqrt(2 * K) / s)
    packed_fT = pack_weight(n((K, W)) / np.sqrt(2 * K) / s)
    return {
        "x_words": packed_xT[0],
        "x_scales": packed_xT[1],
        "e_words": packed_eT[0],
        "e_scales": packed_eT[1],
        "f_words": packed_fT[0],
        "f_scales": packed_fT[1],
        "hT": (n((K, S)) * s).astype(np.float32),
        "offs": striped(np.random.permutation(T)[:S]),
        "cand": striped(np.random.permutation(W)[:V]),
    }


def reference(x_words, x_scales, e_words, e_scales, f_words, f_scales, hT, offs, cand):
    xq = unpack_weight(x_words, x_scales)[:, unstriped(offs)]
    e_cand = unpack_weight(e_words, e_scales)[:, unstriped(cand)]
    hTq = mxq(f64(hT), 0, "e4m3")
    f_cand = unpack_weight(f_words, f_scales)[:, unstriped(cand)]
    y = xq.T @ e_cand + hTq.T @ f_cand
    return sigmoid(y)

@@ -1,0 +1,169 @@
+from contextlib import ExitStack
+
+import concourse.mybir as mybir
+
+K, T, S, V, W = 512, 1024, 512, 512, 2048
+FLOPS = 2 * 2 * K * S * V
+
+F32 = mybir.dt.float32
+BF16 = mybir.dt.bfloat16
+I32 = mybir.dt.int32
+U32 = mybir.dt.uint32
+U16 = mybir.dt.uint16
+U8 = mybir.dt.uint8
+FP8X4 = mybir.dt.float8_e4m3fn_x4
+SIGMOID = mybir.ActivationFunctionType.Sigmoid
+
+P = 128
+PACK = 4
+M_TILE = 128
+N_HALF = 256
+X_ROW, E_ROW, F_ROW = 0, 4, 8
+H_CHUNKS = (256, 128, 128)
+
+KB = 1024
+XS_TABLE = 4 * KB - 512
+FW_TABLE = 4 * KB
+XW_TABLE = 13 * KB
+ES = 18 * KB
+H_RAW = (0, 12 * KB, 15 * KB)
+EW_TABLE = 18 * KB
+FS = 26 * KB
+ES_TABLE = 26 * KB
+FS_TABLE = 28 * KB
+XS = 30 * KB
+XW = 31 * KB
+EW = 33 * KB
+FW = 35 * KB
+
+
+def tile_picked_zsess_sigmoid_p_kernel(
+    tc, x_words, x_scales, e_words, e_scales, f_words, f_scales, hT, offs, cand, out
+):
+    nc = tc.nc
+    with ExitStack() as ctx:
+        lists = ctx.enter_context(tc.tile_pool(name="lists", bufs=1))
+        tables = ctx.enter_context(tc.tile_pool(name="tables", bufs=1))
+        keep = ctx.enter_context(tc.tile_pool(name="keep", bufs=1))
+        psum = ctx.enter_context(tc.psum_pool(name="psum", bufs=1))
+
+        offs_sb = lists.tile([P, S // 16], U16, name="offs_sb")
+        cand_sb = lists.tile([P, V // 16], U16, name="cand_sb")
+
+        def load_words(words, width, name, offset):
+            table = tables.tile([P, width], I32, name=name, offset=offset, align_bytes=64)
+            nc.sync.dma_start(table[:], words[0].rearrange("p n t -> p (n t)").bitcast(I32))
+            return table
+
+        def clear_scales(width, name, offset):
+            table = tables.tile([P, width], U8, name=name, offset=offset, align_bytes=64)
+            nc.vector.memset(table[:].bitcast(I32), 0)
+            return table
+
+        def load_scales(queue, table, scales, first_row, quadrants):
+            for q in quadrants:
+                rows = slice(32 * q + first_row, 32 * q + first_row + 4)
+                queue.dma_start(table[rows, :].bitcast(I32), scales[0, 4 * q : 4 * q + 4, :].bitcast(I32))
+
+        def load_h(c, offset):
+            t0 = sum(H_CHUNKS[:c])
+            raw = tables.tile([P, PACK, H_CHUNKS[c]], F32, name="h_raw%d" % c, offset=offset, align_bytes=64)
+            nc.sync.dma_start(raw[:], hT[:, t0 : t0 + H_CHUNKS[c]].rearrange("(p j) w -> p j w", j=PACK))
+            return raw
+
+        def gather(table, offsets, dtype, name, offset):
+            picked = tables.tile([P, 16 * offsets.shape[1]], dtype, name=name, offset=offset, align_bytes=64)
+            nc.vector.tensor_copy(picked[:], table.indirect(offsets))
+            return picked
+
+        def interleave(copy, raw, c):
+            grouped = keep.tile([P, H_CHUNKS[c], PACK], BF16, name="h_bf%d" % c, align_bytes=64)
+            copy(
+                grouped[:].rearrange("p (c i) j -> p c j i", i=4),
+                raw[:].rearrange("p j (c i) -> p c j i", i=4),
+            )
+            return grouped
+
+        def quantize(grouped, c):
+            codes = keep.tile([P, H_CHUNKS[c]], U32, name="h_codes%d" % c, align_bytes=64)
+            scales = keep.tile([P, H_CHUNKS[c]], U8, name="h_scales%d" % c, align_bytes=64)
+            nc.vector.quantize_mx(codes[:].bitcast(FP8X4), scales[:], grouped[:].rearrange("p w j -> p (w j)"))
+            return codes, scales
+
+        xs_table = clear_scales(T, "xs_table", XS_TABLE)
+        es_table = clear_scales(W, "es_table", ES_TABLE)
+        fs_table = clear_scales(W, "fs_table", FS_TABLE)
+        warm_in = keep.tile([P, 1], F32, name="warm_in")
+        warm_out = keep.tile([P, 1], F32, name="warm_out")
+        nc.vector.memset(warm_in[:], 0.0)
+
+        nc.sync.dma_start(cand_sb[:], cand)
+        nc.sync.dma_start(offs_sb[:], offs)
+        xw_table = load_words(x_words, T, "xw_table", XW_TABLE)
+        ew_table = load_words(e_words, W, "ew_table", EW_TABLE)
+        load_scales(nc.scalar, xs_table, x_scales, X_ROW, range(4))
+        load_scales(nc.scalar, es_table, e_scales, E_ROW, range(4))
+        load_scales(nc.scalar, fs_table, f_scales, F_ROW, range(4))
+        nc.scalar.activation(warm_out[:], warm_in[:], SIGMOID)
+
+        xs = gather(xs_table[:], offs_sb[:], U8, "xs", XS)
+        h_raw0 = load_h(0, H_RAW[0])
+        fw_table = load_words(f_words, W, "fw_table", FW_TABLE)
+        xw = gather(xw_table[:].bitcast(U32), offs_sb[:], U32, "xw", XW)
+        h_raw1 = load_h(1, H_RAW[1])
+        h_raw2 = load_h(2, H_RAW[2])
+        ew = gather(ew_table[:].bitcast(U32), cand_sb[:], U32, "ew", EW)
+        es = gather(es_table[:], cand_sb[:], U8, "es", ES)
+        fs = gather(fs_table[:], cand_sb[:], U8, "fs", FS)
+
+        acc = {}
+        for b in range(V // N_HALF):
+            for i in range(S // M_TILE):
+                acc[i, b] = psum.tile([M_TILE, N_HALF], F32, name="acc%d_%d" % (i, b))
+                users = slice(i * M_TILE, (i + 1) * M_TILE)
+                items = slice(b * N_HALF, (b + 1) * N_HALF)
+                nc.tensor.matmul_mx(
+                    acc[i, b][:],
+                    lhsT=xw[:, users].bitcast(FP8X4),
+                    lhsT_scale=xs[X_ROW:, users],
+                    rhs=ew[:, items].bitcast(FP8X4),
+                    rhs_scale=es[E_ROW:, items],
+                    start=True,
+                    stop=False,
+                )
+
+        result = [keep.tile([M_TILE, V], F32, name="result%d" % i) for i in range(S // M_TILE)]
+
+        def finish(i, b, codes, scales, local, fw_half):
+            users = slice(local * M_TILE, (local + 1) * M_TILE)
+            items = slice(b * N_HALF, (b + 1) * N_HALF)
+            nc.tensor.matmul_mx(
+                acc[i, b][:],
+                lhsT=codes[:, users].bitcast(FP8X4),
+                lhsT_scale=scales[:, users],
+                rhs=fw_half[:].bitcast(FP8X4),
+                rhs_scale=fs[F_ROW:, items],
+                start=False,
+                stop=True,
+            )
+            nc.scalar.activation(result[i][:, items], acc[i, b][:], SIGMOID)
+
+        def store(i):
+            nc.sync.dma_start(out[i * M_TILE : (i + 1) * M_TILE, :], result[i][:])
+
+        codes0, scales0 = quantize(interleave(nc.scalar.copy, h_raw0, 0), 0)
+        fw = []
+        for b in range(V // N_HALF):
+            cols = slice(b * N_HALF // 16, (b + 1) * N_HALF // 16)
+            fw.append(gather(fw_table[:].bitcast(U32), cand_sb[:, cols], U32, "fw%d" % b, FW + 1024 * b))
+            for i in range(2):
+                finish(i, b, codes0, scales0, i, fw[b])
+        store(0)
+        store(1)
+        grouped1 = interleave(nc.vector.tensor_copy, h_raw1, 1)
+        grouped2 = interleave(nc.vector.tensor_copy, h_raw2, 2)
+        for c, grouped in ((1, grouped1), (2, grouped2)):
+            codes, scales = quantize(grouped, c)
+            for b in range(V // N_HALF):
+                finish(c + 1, b, codes, scales, 0, fw[b])
+            store(c + 1)

@@ -21,21 +21,6 @@ N_HALF = 256
 X_ROW, E_ROW, F_ROW = 0, 4, 8
 H_CHUNKS = (256, 128, 128)
 
-KB = 1024
-XS_TABLE = 4 * KB - 512
-FW_TABLE = 4 * KB
-XW_TABLE = 13 * KB
-ES = 18 * KB
-H_RAW = (0, 12 * KB, 15 * KB)
-EW_TABLE = 18 * KB
-FS = 26 * KB
-ES_TABLE = 26 * KB
-FS_TABLE = 28 * KB
-XS = 30 * KB
-XW = 31 * KB
-EW = 33 * KB
-FW = 35 * KB
-
 
 def tile_picked_zsess_sigmoid_p_kernel(
     tc, x_words, x_scales, e_words, e_scales, f_words, f_scales, hT, offs, cand, out
@@ -50,13 +35,13 @@ def tile_picked_zsess_sigmoid_p_kernel(
         offs_sb = lists.tile([P, S // 16], U16, name="offs_sb")
         cand_sb = lists.tile([P, V // 16], U16, name="cand_sb")
 
-        def load_words(words, width, name, offset):
-            table = tables.tile([P, width], I32, name=name, offset=offset, align_bytes=64)
+        def load_words(words, width, name):
+            table = tables.tile([P, width], I32, name=name, align_bytes=64)
             nc.sync.dma_start(table[:], words[0].rearrange("p n t -> p (n t)").bitcast(I32))
             return table
 
-        def clear_scales(width, name, offset):
-            table = tables.tile([P, width], U8, name=name, offset=offset, align_bytes=64)
+        def clear_scales(width, name):
+            table = tables.tile([P, width], U8, name=name, align_bytes=64)
             nc.vector.memset(table[:].bitcast(I32), 0)
             return table
 
@@ -65,14 +50,14 @@ def tile_picked_zsess_sigmoid_p_kernel(
                 rows = slice(32 * q + first_row, 32 * q + first_row + 4)
                 queue.dma_start(table[rows, :].bitcast(I32), scales[0, 4 * q : 4 * q + 4, :].bitcast(I32))
 
-        def load_h(c, offset):
+        def load_h(c):
             t0 = sum(H_CHUNKS[:c])
-            raw = tables.tile([P, PACK, H_CHUNKS[c]], F32, name="h_raw%d" % c, offset=offset, align_bytes=64)
+            raw = tables.tile([P, PACK, H_CHUNKS[c]], F32, name="h_raw%d" % c, tag="h_raw%d" % c, align_bytes=64)
             nc.sync.dma_start(raw[:], hT[:, t0 : t0 + H_CHUNKS[c]].rearrange("(p j) w -> p j w", j=PACK))
             return raw
 
-        def gather(table, offsets, dtype, name, offset):
-            picked = tables.tile([P, 16 * offsets.shape[1]], dtype, name=name, offset=offset, align_bytes=64)
+        def gather(table, offsets, dtype, name):
+            picked = tables.tile([P, 16 * offsets.shape[1]], dtype, name=name, align_bytes=64)
             nc.vector.tensor_copy(picked[:], table.indirect(offsets))
             return picked
 
@@ -90,31 +75,32 @@ def tile_picked_zsess_sigmoid_p_kernel(
             nc.vector.quantize_mx(codes[:].bitcast(FP8X4), scales[:], grouped[:].rearrange("p w j -> p (w j)"))
             return codes, scales
 
-        xs_table = clear_scales(T, "xs_table", XS_TABLE)
-        es_table = clear_scales(W, "es_table", ES_TABLE)
-        fs_table = clear_scales(W, "fs_table", FS_TABLE)
+        xs_table = clear_scales(T, "xs_table")
+        es_table = clear_scales(W, "es_table")
+        fs_table = clear_scales(W, "fs_table")
         warm_in = keep.tile([P, 1], F32, name="warm_in")
         warm_out = keep.tile([P, 1], F32, name="warm_out")
-        nc.vector.memset(warm_in[:], 0.0)
-
-        nc.sync.dma_start(cand_sb[:], cand)
-        nc.sync.dma_start(offs_sb[:], offs)
-        xw_table = load_words(x_words, T, "xw_table", XW_TABLE)
-        ew_table = load_words(e_words, W, "ew_table", EW_TABLE)
-        load_scales(nc.scalar, xs_table, x_scales, X_ROW, range(4))
-        load_scales(nc.scalar, es_table, e_scales, E_ROW, range(4))
-        load_scales(nc.scalar, fs_table, f_scales, F_ROW, range(4))
+        nc.gpsimd.memset(warm_in[:], 0.0)
         nc.scalar.activation(warm_out[:], warm_in[:], SIGMOID)
 
-        xs = gather(xs_table[:], offs_sb[:], U8, "xs", XS)
-        h_raw0 = load_h(0, H_RAW[0])
-        fw_table = load_words(f_words, W, "fw_table", FW_TABLE)
-        xw = gather(xw_table[:].bitcast(U32), offs_sb[:], U32, "xw", XW)
-        h_raw1 = load_h(1, H_RAW[1])
-        h_raw2 = load_h(2, H_RAW[2])
-        ew = gather(ew_table[:].bitcast(U32), cand_sb[:], U32, "ew", EW)
-        es = gather(es_table[:], cand_sb[:], U8, "es", ES)
-        fs = gather(fs_table[:], cand_sb[:], U8, "fs", FS)
+        xw_table = load_words(x_words, T, "xw_table")
+        nc.sync.dma_start(offs_sb[:], offs)
+        nc.sync.dma_start(cand_sb[:], cand)
+        load_scales(nc.sync, xs_table, x_scales, X_ROW, range(4))
+        ew_table = load_words(e_words, W, "ew_table")
+        load_scales(nc.sync, es_table, e_scales, E_ROW, range(4))
+        load_scales(nc.sync, fs_table, f_scales, F_ROW, range(2))
+        h_raw0 = load_h(0)
+        load_scales(nc.sync, fs_table, f_scales, F_ROW, range(2, 4))
+        fw_table = load_words(f_words, W, "fw_table")
+        h_raw1 = load_h(1)
+        h_raw2 = load_h(2)
+
+        xw = gather(xw_table[:].bitcast(U32), offs_sb[:], U32, "xw")
+        xs = gather(xs_table[:], offs_sb[:], U8, "xs")
+        ew = gather(ew_table[:].bitcast(U32), cand_sb[:], U32, "ew")
+        es = gather(es_table[:], cand_sb[:], U8, "es")
+        fs = gather(fs_table[:], cand_sb[:], U8, "fs")
 
         acc = {}
         for b in range(V // N_HALF):
@@ -132,8 +118,6 @@ def tile_picked_zsess_sigmoid_p_kernel(
                     stop=False,
                 )
 
-        result = [keep.tile([M_TILE, V], F32, name="result%d" % i) for i in range(S // M_TILE)]
-
         def finish(i, b, codes, scales, local, fw_half):
             users = slice(local * M_TILE, (local + 1) * M_TILE)
             items = slice(b * N_HALF, (b + 1) * N_HALF)
@@ -146,24 +130,21 @@ def tile_picked_zsess_sigmoid_p_kernel(
                 start=False,
                 stop=True,
             )
-            nc.scalar.activation(result[i][:, items], acc[i, b][:], SIGMOID)
-
-        def store(i):
-            nc.sync.dma_start(out[i * M_TILE : (i + 1) * M_TILE, :], result[i][:])
+            tag = "h_raw1" if (i, b) == (0, 0) else "result%d_%d" % (i, b)
+            result = tables.tile([M_TILE, N_HALF], F32, name="result%d_%d" % (i, b), tag=tag, align_bytes=64)
+            nc.scalar.activation(result[:], acc[i, b][:], SIGMOID)
+            nc.sync.dma_start(out[i * M_TILE : (i + 1) * M_TILE, items], result[:])
 
         codes0, scales0 = quantize(interleave(nc.scalar.copy, h_raw0, 0), 0)
+        grouped1 = interleave(nc.scalar.copy, h_raw1, 1)
         fw = []
         for b in range(V // N_HALF):
             cols = slice(b * N_HALF // 16, (b + 1) * N_HALF // 16)
-            fw.append(gather(fw_table[:].bitcast(U32), cand_sb[:, cols], U32, "fw%d" % b, FW + 1024 * b))
+            fw.append(gather(fw_table[:].bitcast(U32), cand_sb[:, cols], U32, "fw%d" % b))
             for i in range(2):
                 finish(i, b, codes0, scales0, i, fw[b])
-        store(0)
-        store(1)
-        grouped1 = interleave(nc.vector.tensor_copy, h_raw1, 1)
         grouped2 = interleave(nc.vector.tensor_copy, h_raw2, 2)
         for c, grouped in ((1, grouped1), (2, grouped2)):
             codes, scales = quantize(grouped, c)
             for b in range(V // N_HALF):
                 finish(c + 1, b, codes, scales, 0, fw[b])
-            store(c + 1)

@@ -45,10 +45,8 @@ def tile_picked_zsess_sigmoid_p_kernel(
             nc.vector.memset(table[:].bitcast(I32), 0)
             return table
 
-        def load_scales(queue, table, scales, first_row, quadrants):
-            for q in quadrants:
-                rows = slice(32 * q + first_row, 32 * q + first_row + 4)
-                queue.dma_start(table[rows, :].bitcast(I32), scales[0, 4 * q : 4 * q + 4, :].bitcast(I32))
+        def load_scales(table, scales, first_row, r):
+            nc.sync.dma_start(table[first_row + r : P : 32, :].bitcast(I32), scales[0, r:16:4, :].bitcast(I32))
 
         def load_h(c):
             t0 = sum(H_CHUNKS[:c])
@@ -86,12 +84,16 @@ def tile_picked_zsess_sigmoid_p_kernel(
         xw_table = load_words(x_words, T, "xw_table")
         nc.sync.dma_start(offs_sb[:], offs)
         nc.sync.dma_start(cand_sb[:], cand)
-        load_scales(nc.sync, xs_table, x_scales, X_ROW, range(4))
+        for r in range(4):
+            load_scales(xs_table, x_scales, X_ROW, r)
         ew_table = load_words(e_words, W, "ew_table")
-        load_scales(nc.sync, es_table, e_scales, E_ROW, range(4))
-        load_scales(nc.sync, fs_table, f_scales, F_ROW, range(2))
+        for r in range(4):
+            load_scales(es_table, e_scales, E_ROW, r)
+            if r < 2:
+                load_scales(fs_table, f_scales, F_ROW, r)
         h_raw0 = load_h(0)
-        load_scales(nc.sync, fs_table, f_scales, F_ROW, range(2, 4))
+        for r in range(2, 4):
+            load_scales(fs_table, f_scales, F_ROW, r)
         fw_table = load_words(f_words, W, "fw_table")
         h_raw1 = load_h(1)
         h_raw2 = load_h(2)

@@ -16,10 +16,16 @@ SIGMOID = mybir.ActivationFunctionType.Sigmoid
 
 P = 128
 PACK = 4
+QUADRANT = 32
+ROWS = 4
+LIST_COLUMN = 16
+RUN = 4
 M_TILE = 128
 N_HALF = 256
+H_HALF = 256
+ALIGN = 64
+
 X_ROW, E_ROW, F_ROW = 0, 4, 8
-H_CHUNKS = (256, 128, 128)
 
 
 def tile_picked_zsess_sigmoid_p_kernel(
@@ -32,71 +38,70 @@ def tile_picked_zsess_sigmoid_p_kernel(
         keep = ctx.enter_context(tc.tile_pool(name="keep", bufs=1))
         psum = ctx.enter_context(tc.psum_pool(name="psum", bufs=1))
 
-        offs_sb = lists.tile([P, S // 16], U16, name="offs_sb")
-        cand_sb = lists.tile([P, V // 16], U16, name="cand_sb")
+        offs_sb = lists.tile([P, S // LIST_COLUMN], U16, name="offs_sb")
+        cand_sb = lists.tile([P, V // LIST_COLUMN], U16, name="cand_sb")
 
-        def load_words(words, width, name):
-            table = tables.tile([P, width], I32, name=name, align_bytes=64)
+        def load_words(words, columns, name):
+            table = tables.tile([P, columns], I32, name=name, align_bytes=ALIGN)
             nc.sync.dma_start(table[:], words[0].rearrange("p n t -> p (n t)").bitcast(I32))
             return table
 
-        def clear_scales(width, name):
-            table = tables.tile([P, width], U8, name=name, align_bytes=64)
+        def zeroed_scale_table(columns, name):
+            table = tables.tile([P, columns], U8, name=name, align_bytes=ALIGN)
             nc.vector.memset(table[:].bitcast(I32), 0)
             return table
 
-        def load_scales(table, scales, first_row, r):
-            nc.sync.dma_start(table[first_row + r : P : 32, :].bitcast(I32), scales[0, r:16:4, :].bitcast(I32))
+        def load_scale_rows(table, scales, first_row, r):
+            nc.sync.dma_start(
+                table[first_row + r : P : QUADRANT, :].bitcast(I32),
+                scales[0, r : K // 32 : ROWS, :].bitcast(I32),
+            )
 
-        def load_h(c):
-            t0 = sum(H_CHUNKS[:c])
-            raw = tables.tile([P, PACK, H_CHUNKS[c]], F32, name="h_raw%d" % c, tag="h_raw%d" % c, align_bytes=64)
-            nc.sync.dma_start(raw[:], hT[:, t0 : t0 + H_CHUNKS[c]].rearrange("(p j) w -> p j w", j=PACK))
+        def load_h(half):
+            raw = tables.tile([P, PACK, H_HALF], F32, name="h_raw%d" % half, align_bytes=ALIGN)
+            users = slice(half * H_HALF, (half + 1) * H_HALF)
+            nc.sync.dma_start(raw[:], hT[:, users].rearrange("(p j) t -> p j t", j=PACK))
             return raw
 
         def gather(table, offsets, dtype, name):
-            picked = tables.tile([P, 16 * offsets.shape[1]], dtype, name=name, align_bytes=64)
+            picked = tables.tile([P, LIST_COLUMN * offsets.shape[1]], dtype, name=name, align_bytes=ALIGN)
             nc.vector.tensor_copy(picked[:], table.indirect(offsets))
             return picked
 
-        def interleave(copy, raw, c):
-            grouped = keep.tile([P, H_CHUNKS[c], PACK], BF16, name="h_bf%d" % c, align_bytes=64)
+        def cast(copy, raw, name):
+            grouped = keep.tile([P, raw.shape[2], PACK], BF16, name=name, align_bytes=ALIGN)
             copy(
-                grouped[:].rearrange("p (c i) j -> p c j i", i=4),
-                raw[:].rearrange("p j (c i) -> p c j i", i=4),
+                grouped[:].rearrange("p (c i) j -> p c j i", i=RUN),
+                raw.rearrange("p j (c i) -> p c j i", i=RUN),
             )
             return grouped
 
-        def quantize(grouped, c):
-            codes = keep.tile([P, H_CHUNKS[c]], U32, name="h_codes%d" % c, align_bytes=64)
-            scales = keep.tile([P, H_CHUNKS[c]], U8, name="h_scales%d" % c, align_bytes=64)
-            nc.vector.quantize_mx(codes[:].bitcast(FP8X4), scales[:], grouped[:].rearrange("p w j -> p (w j)"))
+        def quantize(grouped, name):
+            users = grouped.shape[1]
+            codes = keep.tile([P, users], U32, name=name + "_codes", align_bytes=ALIGN)
+            scales = keep.tile([P, users], U8, name=name + "_scales", align_bytes=ALIGN)
+            nc.vector.quantize_mx(codes[:].bitcast(FP8X4), scales[:], grouped[:].rearrange("p t j -> p (t j)"))
             return codes, scales
 
-        xs_table = clear_scales(T, "xs_table")
-        es_table = clear_scales(W, "es_table")
-        fs_table = clear_scales(W, "fs_table")
-        warm_in = keep.tile([P, 1], F32, name="warm_in")
-        warm_out = keep.tile([P, 1], F32, name="warm_out")
-        nc.gpsimd.memset(warm_in[:], 0.0)
-        nc.scalar.activation(warm_out[:], warm_in[:], SIGMOID)
+        xs_table = zeroed_scale_table(T, "xs_table")
+        es_table = zeroed_scale_table(W, "es_table")
+        fs_table = zeroed_scale_table(W, "fs_table")
 
         xw_table = load_words(x_words, T, "xw_table")
         nc.sync.dma_start(offs_sb[:], offs)
         nc.sync.dma_start(cand_sb[:], cand)
-        for r in range(4):
-            load_scales(xs_table, x_scales, X_ROW, r)
+        for r in range(ROWS):
+            load_scale_rows(xs_table, x_scales, X_ROW, r)
         ew_table = load_words(e_words, W, "ew_table")
-        for r in range(4):
-            load_scales(es_table, e_scales, E_ROW, r)
-            if r < 2:
-                load_scales(fs_table, f_scales, F_ROW, r)
-        h_raw0 = load_h(0)
-        for r in range(2, 4):
-            load_scales(fs_table, f_scales, F_ROW, r)
+        for r in range(ROWS):
+            load_scale_rows(es_table, e_scales, E_ROW, r)
+            if r < ROWS // 2:
+                load_scale_rows(fs_table, f_scales, F_ROW, r)
+        h_early = load_h(0)
+        for r in range(ROWS // 2, ROWS):
+            load_scale_rows(fs_table, f_scales, F_ROW, r)
         fw_table = load_words(f_words, W, "fw_table")
-        h_raw1 = load_h(1)
-        h_raw2 = load_h(2)
+        h_late = load_h(1)
 
         xw = gather(xw_table[:].bitcast(U32), offs_sb[:], U32, "xw")
         xs = gather(xs_table[:], offs_sb[:], U8, "xs")
@@ -120,33 +125,36 @@ def tile_picked_zsess_sigmoid_p_kernel(
                     stop=False,
                 )
 
-        def finish(i, b, codes, scales, local, fw_half):
-            users = slice(local * M_TILE, (local + 1) * M_TILE)
+        def finish(i, b, h_codes, h_scales, fw_half):
             items = slice(b * N_HALF, (b + 1) * N_HALF)
             nc.tensor.matmul_mx(
                 acc[i, b][:],
-                lhsT=codes[:, users].bitcast(FP8X4),
-                lhsT_scale=scales[:, users],
+                lhsT=h_codes.bitcast(FP8X4),
+                lhsT_scale=h_scales,
                 rhs=fw_half[:].bitcast(FP8X4),
                 rhs_scale=fs[F_ROW:, items],
                 start=False,
                 stop=True,
             )
-            tag = "h_raw1" if (i, b) == (0, 0) else "result%d_%d" % (i, b)
-            result = tables.tile([M_TILE, N_HALF], F32, name="result%d_%d" % (i, b), tag=tag, align_bytes=64)
+            result = tables.tile([M_TILE, N_HALF], F32, name="result%d_%d" % (i, b))
             nc.scalar.activation(result[:], acc[i, b][:], SIGMOID)
             nc.sync.dma_start(out[i * M_TILE : (i + 1) * M_TILE, items], result[:])
 
-        codes0, scales0 = quantize(interleave(nc.scalar.copy, h_raw0, 0), 0)
-        grouped1 = interleave(nc.scalar.copy, h_raw1, 1)
+        tiles_in_half = H_HALF // M_TILE
+        early_codes, early_scales = quantize(cast(nc.scalar.copy, h_early[:], "h_early_bf"), "h_early")
         fw = []
         for b in range(V // N_HALF):
-            cols = slice(b * N_HALF // 16, (b + 1) * N_HALF // 16)
-            fw.append(gather(fw_table[:].bitcast(U32), cand_sb[:, cols], U32, "fw%d" % b))
-            for i in range(2):
-                finish(i, b, codes0, scales0, i, fw[b])
-        grouped2 = interleave(nc.vector.tensor_copy, h_raw2, 2)
-        for c, grouped in ((1, grouped1), (2, grouped2)):
-            codes, scales = quantize(grouped, c)
+            columns = slice(b * N_HALF // LIST_COLUMN, (b + 1) * N_HALF // LIST_COLUMN)
+            fw.append(gather(fw_table[:].bitcast(U32), cand_sb[:, columns], U32, "fw%d" % b))
+            for i in range(tiles_in_half):
+                users = slice(i * M_TILE, (i + 1) * M_TILE)
+                finish(i, b, early_codes[:, users], early_scales[:, users], fw[b])
+
+        late = []
+        for i in range(tiles_in_half):
+            raw = h_late[:, :, i * M_TILE : (i + 1) * M_TILE]
+            late.append(cast(nc.vector.tensor_copy, raw, "h_late_bf%d" % i))
+        for i in range(tiles_in_half):
+            late_codes, late_scales = quantize(late[i], "h_late%d" % i)
             for b in range(V // N_HALF):
-                finish(c + 1, b, codes, scales, 0, fw[b])
+                finish(tiles_in_half + i, b, late_codes[:], late_scales[:], fw[b])

@@ -87,6 +87,11 @@ def tile_picked_zsess_sigmoid_p_kernel(
         es_table = zeroed_scale_table(W, "es_table")
         fs_table = zeroed_scale_table(W, "fs_table")
 
+        warm_in = keep.tile([P, 1], F32, name="warm_in")
+        warm_out = keep.tile([P, 1], F32, name="warm_out")
+        nc.gpsimd.memset(warm_in[:], 0.0)
+        nc.scalar.activation(warm_out[:], warm_in[:], SIGMOID)
+
         xw_table = load_words(x_words, T, "xw_table")
         nc.sync.dma_start(offs_sb[:], offs)
         nc.sync.dma_start(cand_sb[:], cand)

@@ -13,6 +13,8 @@ U16 = mybir.dt.uint16
 U8 = mybir.dt.uint8
 FP8X4 = mybir.dt.float8_e4m3fn_x4
 SIGMOID = mybir.ActivationFunctionType.Sigmoid
+MULT = mybir.AluOpType.mult
+ADD = mybir.AluOpType.add
 
 P = 128
 PACK = 4
@@ -22,10 +24,8 @@ LIST_COLUMN = 16
 RUN = 4
 M_TILE = 128
 N_HALF = 256
-H_HALF = 256
 ALIGN = 64
-
-X_ROW, E_ROW, F_ROW = 0, 4, 8
+X_ROW, E_ROW, F_ROW = 8, 4, 0
 
 
 def tile_picked_zsess_sigmoid_p_kernel(
@@ -41,56 +41,73 @@ def tile_picked_zsess_sigmoid_p_kernel(
         offs_sb = lists.tile([P, S // LIST_COLUMN], U16, name="offs_sb")
         cand_sb = lists.tile([P, V // LIST_COLUMN], U16, name="cand_sb")
 
-        def load_words(words, columns, name):
+        def load_words(words, columns, name, queue=nc.sync):
             table = tables.tile([P, columns], I32, name=name, align_bytes=ALIGN)
-            nc.sync.dma_start(table[:], words[0].rearrange("p n t -> p (n t)").bitcast(I32))
+            queue.dma_start(table[:], words[0].rearrange("p n t -> p (n t)").bitcast(I32))
             return table
 
-        def zeroed_scale_table(columns, name):
+        def zeroed_scale_table(columns, name, engine=nc.vector):
             table = tables.tile([P, columns], U8, name=name, align_bytes=ALIGN)
-            nc.vector.memset(table[:].bitcast(I32), 0)
+            engine.memset(table[:].bitcast(I32), 0)
             return table
 
-        def load_scale_rows(table, scales, first_row, r):
-            nc.sync.dma_start(
+        def load_scale_rows(table, scales, first_row, r, queue=nc.sync):
+            queue.dma_start(
                 table[first_row + r : P : QUADRANT, :].bitcast(I32),
                 scales[0, r : K // 32 : ROWS, :].bitcast(I32),
             )
 
-        def load_h(half):
-            raw = tables.tile([P, PACK, H_HALF], F32, name="h_raw%d" % half, align_bytes=ALIGN)
-            users = slice(half * H_HALF, (half + 1) * H_HALF)
-            nc.sync.dma_start(raw[:], hT[:, users].rearrange("(p j) t -> p j t", j=PACK))
+        def load_h(first, count, queue=nc.sync):
+            raw = tables.tile([P, PACK, count * M_TILE], F32, name="h_raw%d" % first, align_bytes=ALIGN)
+            users = slice(first * M_TILE, (first + count) * M_TILE)
+            queue.dma_start(raw[:], hT[:, users].rearrange("(p j) t -> p j t", j=PACK))
             return raw
 
-        def gather(table, offsets, dtype, name):
-            picked = tables.tile([P, LIST_COLUMN * offsets.shape[1]], dtype, name=name, align_bytes=ALIGN)
+        def gather(table, offsets, dtype, name, tag=None):
+            picked = tables.tile([P, LIST_COLUMN * offsets.shape[1]], dtype, name=name, tag=tag or name, align_bytes=ALIGN)
             nc.vector.tensor_copy(picked[:], table.indirect(offsets))
             return picked
 
-        def cast(copy, raw, name):
-            grouped = keep.tile([P, raw.shape[2], PACK], BF16, name=name, align_bytes=ALIGN)
+        def gp_copy(dst, src):
+            nc.gpsimd.tensor_scalar(dst, src, 1.0, 0.0, MULT, ADD)
+
+        def cast(copy, raw, name, tag=None):
+            grouped = tables.tile([P, raw.shape[2], PACK], BF16, name=name, tag=tag or name, align_bytes=ALIGN)
             copy(
                 grouped[:].rearrange("p (c i) j -> p c j i", i=RUN),
                 raw.rearrange("p j (c i) -> p c j i", i=RUN),
             )
             return grouped
 
-        def quantize(grouped, name):
+        def quantize(grouped, name, tag=None):
             users = grouped.shape[1]
-            codes = keep.tile([P, users], U32, name=name + "_codes", align_bytes=ALIGN)
+            codes = tables.tile([P, users], U32, name=name + "_codes", tag=tag or name, align_bytes=ALIGN)
             scales = keep.tile([P, users], U8, name=name + "_scales", align_bytes=ALIGN)
             nc.vector.quantize_mx(codes[:].bitcast(FP8X4), scales[:], grouped[:].rearrange("p t j -> p (t j)"))
             return codes, scales
 
+        def columns(first, count):
+            return slice(first // LIST_COLUMN, (first + count) // LIST_COLUMN)
+
+        def product(acc, lhs, lhs_scale, rhs, rhs_scale, first):
+            nc.tensor.matmul_mx(
+                acc,
+                lhsT=lhs.bitcast(FP8X4),
+                lhsT_scale=lhs_scale,
+                rhs=rhs.bitcast(FP8X4),
+                rhs_scale=rhs_scale,
+                start=first,
+                stop=not first,
+            )
+
+        def emit(acc, i, items, name, tag=None, queue=nc.sync):
+            result = tables.tile([M_TILE, items.stop - items.start], F32, name=name, tag=tag or name, align_bytes=ALIGN)
+            nc.scalar.activation(result[:], acc, SIGMOID)
+            queue.dma_start(out[i * M_TILE : (i + 1) * M_TILE, items], result[:])
+
         xs_table = zeroed_scale_table(T, "xs_table")
         es_table = zeroed_scale_table(W, "es_table")
         fs_table = zeroed_scale_table(W, "fs_table")
-
-        warm_in = keep.tile([P, 1], F32, name="warm_in")
-        warm_out = keep.tile([P, 1], F32, name="warm_out")
-        nc.gpsimd.memset(warm_in[:], 0.0)
-        nc.scalar.activation(warm_out[:], warm_in[:], SIGMOID)
 
         xw_table = load_words(x_words, T, "xw_table")
         nc.sync.dma_start(offs_sb[:], offs)
@@ -102,11 +119,11 @@ def tile_picked_zsess_sigmoid_p_kernel(
             load_scale_rows(es_table, e_scales, E_ROW, r)
             if r < ROWS // 2:
                 load_scale_rows(fs_table, f_scales, F_ROW, r)
-        h_early = load_h(0)
+        h_early = load_h(0, 2)
         for r in range(ROWS // 2, ROWS):
             load_scale_rows(fs_table, f_scales, F_ROW, r)
         fw_table = load_words(f_words, W, "fw_table")
-        h_late = load_h(1)
+        h_late = load_h(2, 2)
 
         xw = gather(xw_table[:].bitcast(U32), offs_sb[:], U32, "xw")
         xs = gather(xs_table[:], offs_sb[:], U8, "xs")
@@ -115,51 +132,27 @@ def tile_picked_zsess_sigmoid_p_kernel(
         fs = gather(fs_table[:], cand_sb[:], U8, "fs")
 
         acc = {}
-        for b in range(V // N_HALF):
-            for i in range(S // M_TILE):
+        for b in range(2):
+            for i in range(4):
                 acc[i, b] = psum.tile([M_TILE, N_HALF], F32, name="acc%d_%d" % (i, b))
                 users = slice(i * M_TILE, (i + 1) * M_TILE)
                 items = slice(b * N_HALF, (b + 1) * N_HALF)
-                nc.tensor.matmul_mx(
-                    acc[i, b][:],
-                    lhsT=xw[:, users].bitcast(FP8X4),
-                    lhsT_scale=xs[X_ROW:, users],
-                    rhs=ew[:, items].bitcast(FP8X4),
-                    rhs_scale=es[E_ROW:, items],
-                    start=True,
-                    stop=False,
-                )
+                product(acc[i, b][:], xw[:, users], xs[X_ROW:, users], ew[:, items], es[E_ROW:, items], True)
 
-        def finish(i, b, h_codes, h_scales, fw_half):
+        def finish(i, b, codes, scales):
             items = slice(b * N_HALF, (b + 1) * N_HALF)
-            nc.tensor.matmul_mx(
-                acc[i, b][:],
-                lhsT=h_codes.bitcast(FP8X4),
-                lhsT_scale=h_scales,
-                rhs=fw_half[:].bitcast(FP8X4),
-                rhs_scale=fs[F_ROW:, items],
-                start=False,
-                stop=True,
-            )
-            result = tables.tile([M_TILE, N_HALF], F32, name="result%d_%d" % (i, b))
-            nc.scalar.activation(result[:], acc[i, b][:], SIGMOID)
-            nc.sync.dma_start(out[i * M_TILE : (i + 1) * M_TILE, items], result[:])
+            product(acc[i, b][:], codes, scales, fw[b][:], fs[F_ROW:, items], False)
+            emit(acc[i, b][:], i, items, "result%d_%d" % (i, b))
 
-        tiles_in_half = H_HALF // M_TILE
-        early_codes, early_scales = quantize(cast(nc.scalar.copy, h_early[:], "h_early_bf"), "h_early")
+        early = quantize(cast(nc.scalar.copy, h_early[:], "h_early_bf"), "h_early")
         fw = []
-        for b in range(V // N_HALF):
-            columns = slice(b * N_HALF // LIST_COLUMN, (b + 1) * N_HALF // LIST_COLUMN)
-            fw.append(gather(fw_table[:].bitcast(U32), cand_sb[:, columns], U32, "fw%d" % b))
-            for i in range(tiles_in_half):
+        for b in range(2):
+            fw.append(gather(fw_table[:].bitcast(U32), cand_sb[:, columns(b * N_HALF, N_HALF)], U32, "fw%d" % b))
+            for i in range(2):
                 users = slice(i * M_TILE, (i + 1) * M_TILE)
-                finish(i, b, early_codes[:, users], early_scales[:, users], fw[b])
-
-        late = []
-        for i in range(tiles_in_half):
-            raw = h_late[:, :, i * M_TILE : (i + 1) * M_TILE]
-            late.append(cast(nc.vector.tensor_copy, raw, "h_late_bf%d" % i))
-        for i in range(tiles_in_half):
-            late_codes, late_scales = quantize(late[i], "h_late%d" % i)
-            for b in range(V // N_HALF):
-                finish(tiles_in_half + i, b, late_codes[:], late_scales[:], fw[b])
+                finish(i, b, early[0][:, users], early[1][:, users])
+        late = [cast(nc.vector.tensor_copy, h_late[:, :, i * M_TILE : (i + 1) * M_TILE], "h_late_bf%d" % i) for i in range(2)]
+        for i in range(2):
+            q = quantize(late[i], "h_late%d" % i)
+            for b in range(2):
+                finish(2 + i, b, q[0][:], q[1][:])

@@ -20,12 +20,13 @@ P = 128
 PACK = 4
 QUADRANT = 32
 ROWS = 4
+SPREAD = 8
 LIST_COLUMN = 16
 RUN = 4
 M_TILE = 128
 N_HALF = 256
 ALIGN = 64
-X_ROW, E_ROW, F_ROW = 8, 4, 0
+X_ROW = 8
 
 
 def tile_picked_zsess_sigmoid_p_kernel(
@@ -36,40 +37,53 @@ def tile_picked_zsess_sigmoid_p_kernel(
         lists = ctx.enter_context(tc.tile_pool(name="lists", bufs=1))
         tables = ctx.enter_context(tc.tile_pool(name="tables", bufs=1))
         keep = ctx.enter_context(tc.tile_pool(name="keep", bufs=1))
+        placed = ctx.enter_context(tc.tile_pool(name="placed", bufs=1))
         psum = ctx.enter_context(tc.psum_pool(name="psum", bufs=1))
 
         offs_sb = lists.tile([P, S // LIST_COLUMN], U16, name="offs_sb")
         cand_sb = lists.tile([P, V // LIST_COLUMN], U16, name="cand_sb")
 
-        def load_words(words, columns, name, queue=nc.sync):
-            table = tables.tile([P, columns], I32, name=name, align_bytes=ALIGN)
-            queue.dma_start(table[:], words[0].rearrange("p n t -> p (n t)").bitcast(I32))
+        def tile_at(shape, dtype, name, at=None, tag=None):
+            if at is None:
+                return tables.tile(shape, dtype, name=name, tag=tag or name, align_bytes=ALIGN)
+            return placed.tile(shape, dtype, name=name, offset=at, align_bytes=ALIGN)
+
+        def load_words(words, columns, name, at=None):
+            table = tile_at([P, columns], I32, name, at)
+            nc.sync.dma_start(table[:], words[0].rearrange("p n t -> p (n t)").bitcast(I32))
             return table
 
-        def zeroed_scale_table(columns, name, engine=nc.vector):
-            table = tables.tile([P, columns], U8, name=name, align_bytes=ALIGN)
+        def zeroed(columns, name, engine=nc.vector, at=None):
+            table = tile_at([P, columns], U8, name, at)
             engine.memset(table[:].bitcast(I32), 0)
             return table
 
-        def load_scale_rows(table, scales, first_row, r, queue=nc.sync):
-            queue.dma_start(
+        def load_spread(table, scales, first=0):
+            nc.sync.dma_start(table[first:P:SPREAD, :].bitcast(I32), scales[0].bitcast(I32))
+
+        def load_scale_rows(table, scales, first_row, r):
+            nc.sync.dma_start(
                 table[first_row + r : P : QUADRANT, :].bitcast(I32),
                 scales[0, r : K // 32 : ROWS, :].bitcast(I32),
             )
 
-        def load_h(first, count, queue=nc.sync):
-            raw = tables.tile([P, PACK, count * M_TILE], F32, name="h_raw%d" % first, align_bytes=ALIGN)
+        def move_rows(plane, spread, r, first=0, queue=nc.sync):
+            queue.dma_start(
+                plane[r:P:QUADRANT].bitcast(I32),
+                spread[first + SPREAD * r : P : QUADRANT].bitcast(I32),
+            )
+
+        def load_h(first, count, at=None):
+            name = "h_raw%d" % first
+            raw = tile_at([P, PACK, count * M_TILE], F32, name, at)
             users = slice(first * M_TILE, (first + count) * M_TILE)
-            queue.dma_start(raw[:], hT[:, users].rearrange("(p j) t -> p j t", j=PACK))
+            nc.sync.dma_start(raw[:], hT[:, users].rearrange("(p j) t -> p j t", j=PACK))
             return raw
 
         def gather(table, offsets, dtype, name, tag=None):
             picked = tables.tile([P, LIST_COLUMN * offsets.shape[1]], dtype, name=name, tag=tag or name, align_bytes=ALIGN)
             nc.vector.tensor_copy(picked[:], table.indirect(offsets))
             return picked
-
-        def gp_copy(dst, src):
-            nc.gpsimd.tensor_scalar(dst, src, 1.0, 0.0, MULT, ADD)
 
         def cast(copy, raw, name, tag=None):
             grouped = tables.tile([P, raw.shape[2], PACK], BF16, name=name, tag=tag or name, align_bytes=ALIGN)
@@ -89,6 +103,9 @@ def tile_picked_zsess_sigmoid_p_kernel(
         def columns(first, count):
             return slice(first // LIST_COLUMN, (first + count) // LIST_COLUMN)
 
+        def span(i, n):
+            return slice(i * n, (i + 1) * n)
+
         def product(acc, lhs, lhs_scale, rhs, rhs_scale, first):
             nc.tensor.matmul_mx(
                 acc,
@@ -105,53 +122,63 @@ def tile_picked_zsess_sigmoid_p_kernel(
             nc.scalar.activation(result[:], acc, SIGMOID)
             queue.dma_start(out[i * M_TILE : (i + 1) * M_TILE, items], result[:])
 
-        xs_table = zeroed_scale_table(T, "xs_table")
-        es_table = zeroed_scale_table(W, "es_table")
-        fs_table = zeroed_scale_table(W, "fs_table")
 
-        xw_table = load_words(x_words, T, "xw_table")
+        xs_table = zeroed(T, "xs_table")
+        es_table = zeroed(W, "es_table")
+        fs_table = zeroed(W, "fs_table")
+        plane = zeroed(S + 2 * V, "plane")
+        xw_table = tile_at([P, T], I32, "xw_table")
+        fw_table = tile_at([P, W], I32, "fw_table")
+        x_rows = x_words[0].rearrange("p n t -> p (n t)").bitcast(I32)
+        f_rows = f_words[0].rearrange("p n t -> p (n t)").bitcast(I32)
+        f_split = W // 2
+
+        nc.sync.dma_start(xw_table[:, : T // 2], x_rows[:, : T // 2])
         nc.sync.dma_start(offs_sb[:], offs)
+        load_spread(xs_table, x_scales)
+        nc.sync.dma_start(xw_table[:, T // 2 :], x_rows[:, T // 2 :])
+        load_spread(es_table, e_scales)
+        load_spread(fs_table, f_scales)
         nc.sync.dma_start(cand_sb[:], cand)
-        for r in range(ROWS):
-            load_scale_rows(xs_table, x_scales, X_ROW, r)
-        ew_table = load_words(e_words, W, "ew_table")
-        for r in range(ROWS):
-            load_scale_rows(es_table, e_scales, E_ROW, r)
-            if r < ROWS // 2:
-                load_scale_rows(fs_table, f_scales, F_ROW, r)
         h_early = load_h(0, 2)
-        for r in range(ROWS // 2, ROWS):
-            load_scale_rows(fs_table, f_scales, F_ROW, r)
-        fw_table = load_words(f_words, W, "fw_table")
+        ew_table = load_words(e_words, W, "ew_table")
+        nc.sync.dma_start(fw_table[:, :f_split], f_rows[:, :f_split])
+
+        spread = tile_at([P, S + 2 * V], U8, "spread")
+        nc.vector.tensor_copy(spread[:, :S], xs_table[:].indirect(offs_sb[:]))
+        nc.vector.tensor_copy(spread[:, S : S + V], es_table[:].indirect(cand_sb[:]))
+        nc.vector.tensor_copy(spread[:, S + V :], fs_table[:].indirect(cand_sb[:]))
+        for r in range(ROWS):
+            move_rows(plane, spread, r)
+        xs, es, fs = plane[:, :S], plane[:, S : S + V], plane[:, S + V :]
+        nc.sync.dma_start(fw_table[:, f_split:], f_rows[:, f_split:])
         h_late = load_h(2, 2)
 
-        xw = gather(xw_table[:].bitcast(U32), offs_sb[:], U32, "xw")
-        xs = gather(xs_table[:], offs_sb[:], U8, "xs")
-        ew = gather(ew_table[:].bitcast(U32), cand_sb[:], U32, "ew")
-        es = gather(es_table[:], cand_sb[:], U8, "es")
-        fs = gather(fs_table[:], cand_sb[:], U8, "fs")
+        xw = gather(xw_table[:].bitcast(U32), offs_sb[:], U32, "xw", tag="es_table")
+        early_bf = cast(nc.scalar.copy, h_early[:], "h_early_bf")
 
         acc = {}
         for b in range(2):
+            items = span(b, N_HALF)
+            ew = gather(ew_table[:].bitcast(U32), cand_sb[:, columns(b * N_HALF, N_HALF)], U32, "ew%d" % b)
             for i in range(4):
                 acc[i, b] = psum.tile([M_TILE, N_HALF], F32, name="acc%d_%d" % (i, b))
-                users = slice(i * M_TILE, (i + 1) * M_TILE)
-                items = slice(b * N_HALF, (b + 1) * N_HALF)
-                product(acc[i, b][:], xw[:, users], xs[X_ROW:, users], ew[:, items], es[E_ROW:, items], True)
+                users = span(i, M_TILE)
+                product(acc[i, b][:], xw[:, users], xs[:, users], ew[:], es[:, items], True)
 
         def finish(i, b, codes, scales):
-            items = slice(b * N_HALF, (b + 1) * N_HALF)
-            product(acc[i, b][:], codes, scales, fw[b][:], fs[F_ROW:, items], False)
+            items = span(b, N_HALF)
+            product(acc[i, b][:], codes, scales, fw[b][:], fs[:, items], False)
             emit(acc[i, b][:], i, items, "result%d_%d" % (i, b))
 
-        early = quantize(cast(nc.scalar.copy, h_early[:], "h_early_bf"), "h_early")
+        early = quantize(early_bf, "h_early", tag="spread")
         fw = []
         for b in range(2):
             fw.append(gather(fw_table[:].bitcast(U32), cand_sb[:, columns(b * N_HALF, N_HALF)], U32, "fw%d" % b))
             for i in range(2):
-                users = slice(i * M_TILE, (i + 1) * M_TILE)
+                users = span(i, M_TILE)
                 finish(i, b, early[0][:, users], early[1][:, users])
-        late = [cast(nc.vector.tensor_copy, h_late[:, :, i * M_TILE : (i + 1) * M_TILE], "h_late_bf%d" % i) for i in range(2)]
+        late = [cast(nc.vector.tensor_copy, h_late[:, :, span(i, M_TILE)], "h_late_bf%d" % i) for i in range(2)]
         for i in range(2):
             q = quantize(late[i], "h_late%d" % i)
             for b in range(2):

@@ -128,21 +128,19 @@ def tile_picked_zsess_sigmoid_p_kernel(
         fs_table = zeroed(W, "fs_table")
         plane = zeroed(S + 2 * V, "plane")
         xw_table = tile_at([P, T], I32, "xw_table")
-        fw_table = tile_at([P, W], I32, "fw_table")
         x_rows = x_words[0].rearrange("p n t -> p (n t)").bitcast(I32)
-        f_rows = f_words[0].rearrange("p n t -> p (n t)").bitcast(I32)
-        f_split = W // 2
+        x_split = 3 * T // 8
 
-        nc.sync.dma_start(xw_table[:, : T // 2], x_rows[:, : T // 2])
+        nc.sync.dma_start(xw_table[:, :x_split], x_rows[:, :x_split])
         nc.sync.dma_start(offs_sb[:], offs)
         load_spread(xs_table, x_scales)
-        nc.sync.dma_start(xw_table[:, T // 2 :], x_rows[:, T // 2 :])
-        load_spread(es_table, e_scales)
-        load_spread(fs_table, f_scales)
+        nc.sync.dma_start(xw_table[:, x_split:], x_rows[:, x_split:])
         nc.sync.dma_start(cand_sb[:], cand)
+        load_spread(es_table, e_scales)
         h_early = load_h(0, 2)
+        load_spread(fs_table, f_scales)
         ew_table = load_words(e_words, W, "ew_table")
-        nc.sync.dma_start(fw_table[:, :f_split], f_rows[:, :f_split])
+        fw_table = load_words(f_words, W, "fw_table")
 
         spread = tile_at([P, S + 2 * V], U8, "spread")
         nc.vector.tensor_copy(spread[:, :S], xs_table[:].indirect(offs_sb[:]))
@@ -151,35 +149,57 @@ def tile_picked_zsess_sigmoid_p_kernel(
         for r in range(ROWS):
             move_rows(plane, spread, r)
         xs, es, fs = plane[:, :S], plane[:, S : S + V], plane[:, S + V :]
-        nc.sync.dma_start(fw_table[:, f_split:], f_rows[:, f_split:])
         h_late = load_h(2, 2)
 
-        xw = gather(xw_table[:].bitcast(U32), offs_sb[:], U32, "xw", tag="es_table")
         early_bf = cast(nc.scalar.copy, h_early[:], "h_early_bf")
+        xw = gather(xw_table[:].bitcast(U32), offs_sb[:, columns(0, 3 * M_TILE)], U32, "xw", tag="h_raw0")
+        x_codes = [xw[:, span(i, M_TILE)] for i in range(3)]
+        early = quantize(early_bf, "h_early")
+        h_codes = [(early[0][:, span(i, M_TILE)], early[1][:, span(i, M_TILE)]) for i in range(2)]
 
         acc = {}
-        for b in range(2):
-            items = span(b, N_HALF)
-            ew = gather(ew_table[:].bitcast(U32), cand_sb[:, columns(b * N_HALF, N_HALF)], U32, "ew%d" % b)
-            for i in range(4):
-                acc[i, b] = psum.tile([M_TILE, N_HALF], F32, name="acc%d_%d" % (i, b))
-                users = span(i, M_TILE)
-                product(acc[i, b][:], xw[:, users], xs[:, users], ew[:], es[:, items], True)
-
-        def finish(i, b, codes, scales):
-            items = span(b, N_HALF)
-            product(acc[i, b][:], codes, scales, fw[b][:], fs[:, items], False)
-            emit(acc[i, b][:], i, items, "result%d_%d" % (i, b))
-
-        early = quantize(early_bf, "h_early", tag="spread")
         fw = []
+        ew = tile_at([P, V], U32, "ew")
+
+        def long_term(i, b, first):
+            product(acc[i, b][:], x_codes[i], xs[:, span(i, M_TILE)], ew[:, span(b, N_HALF)], es[:, span(b, N_HALF)], first)
+
+        def session(i, b, first):
+            product(acc[i, b][:], h_codes[i][0], h_codes[i][1], fw[b][:], fs[:, span(b, N_HALF)], first)
+
+        def leave(i, b):
+            emit(acc[i, b][:], i, span(b, N_HALF), "result%d_%d" % (i, b))
+
+        def bank(i, b):
+            acc[i, b] = psum.tile([M_TILE, N_HALF], F32, name="acc%d_%d" % (i, b), tag="bank%d" % (2 * i + b))
+
+        def piece(i, b):
+            bank(i, b)
+            session(i, b, True)
+            long_term(i, b, False)
+            leave(i, b)
+
         for b in range(2):
-            fw.append(gather(fw_table[:].bitcast(U32), cand_sb[:, columns(b * N_HALF, N_HALF)], U32, "fw%d" % b))
-            for i in range(2):
-                users = span(i, M_TILE)
-                finish(i, b, early[0][:, users], early[1][:, users])
-        late = [cast(nc.vector.tensor_copy, h_late[:, :, span(i, M_TILE)], "h_late_bf%d" % i) for i in range(2)]
+            nc.vector.tensor_copy(ew[:, span(b, N_HALF)], ew_table[:].bitcast(U32).indirect(cand_sb[:, columns(b * N_HALF, N_HALF)]))
         for i in range(2):
-            q = quantize(late[i], "h_late%d" % i)
-            for b in range(2):
-                finish(2 + i, b, q[0][:], q[1][:])
+            bank(i, 0)
+            long_term(i, 0, True)
+        fw.append(gather(fw_table[:].bitcast(U32), cand_sb[:, columns(0, N_HALF)], U32, "fw0"))
+        for i in range(2):
+            session(i, 0, False)
+            leave(i, 0)
+        fw.append(gather(fw_table[:].bitcast(U32), cand_sb[:, columns(N_HALF, N_HALF)], U32, "fw1"))
+        for i in range(2):
+            piece(i, 1)
+
+        late = [cast(nc.vector.tensor_copy, h_late[:, :, span(i, M_TILE)], "h_late_bf%d" % i) for i in range(2)]
+        q = quantize(late[0], "h_late0")
+        h_codes.append((q[0][:], q[1][:]))
+        for b in range(2):
+            piece(2, b)
+        xw3 = gather(xw_table[:].bitcast(U32), offs_sb[:, columns(3 * M_TILE, M_TILE)], U32, "xw3", tag="h_raw2")
+        x_codes.append(xw3[:])
+        q = quantize(late[1], "h_late1")
+        h_codes.append((q[0][:], q[1][:]))
+        for b in range(2):
+            piece(3, b)

@@ -126,10 +126,10 @@ def tile_picked_zsess_sigmoid_p_kernel(
         xs_table = zeroed(T, "xs_table")
         es_table = zeroed(W, "es_table")
         fs_table = zeroed(W, "fs_table")
-        plane = zeroed(S + 2 * V, "plane")
+        plane = tile_at([P, S + 2 * V], U8, "plane")
         xw_table = tile_at([P, T], I32, "xw_table")
         x_rows = x_words[0].rearrange("p n t -> p (n t)").bitcast(I32)
-        x_split = 3 * T // 8
+        x_split = T // 2
 
         nc.sync.dma_start(xw_table[:, :x_split], x_rows[:, :x_split])
         nc.sync.dma_start(offs_sb[:], offs)
@@ -146,14 +146,15 @@ def tile_picked_zsess_sigmoid_p_kernel(
         nc.vector.tensor_copy(spread[:, :S], xs_table[:].indirect(offs_sb[:]))
         nc.vector.tensor_copy(spread[:, S : S + V], es_table[:].indirect(cand_sb[:]))
         nc.vector.tensor_copy(spread[:, S + V :], fs_table[:].indirect(cand_sb[:]))
-        for r in range(ROWS):
+        nc.vector.tensor_copy(plane[:].bitcast(I32), spread[:].bitcast(I32))
+        for r in range(1, ROWS):
             move_rows(plane, spread, r)
         xs, es, fs = plane[:, :S], plane[:, S : S + V], plane[:, S + V :]
         h_late = load_h(2, 2)
 
         early_bf = cast(nc.scalar.copy, h_early[:], "h_early_bf")
-        xw = gather(xw_table[:].bitcast(U32), offs_sb[:, columns(0, 3 * M_TILE)], U32, "xw", tag="h_raw0")
-        x_codes = [xw[:, span(i, M_TILE)] for i in range(3)]
+        xw = gather(xw_table[:].bitcast(U32), offs_sb[:], U32, "xw", tag="h_raw0")
+        x_codes = [xw[:, span(i, M_TILE)] for i in range(4)]
         early = quantize(early_bf, "h_early")
         h_codes = [(early[0][:, span(i, M_TILE)], early[1][:, span(i, M_TILE)]) for i in range(2)]
 
@@ -181,6 +182,16 @@ def tile_picked_zsess_sigmoid_p_kernel(
 
         for b in range(2):
             nc.vector.tensor_copy(ew[:, span(b, N_HALF)], ew_table[:].bitcast(U32).indirect(cand_sb[:, columns(b * N_HALF, N_HALF)]))
+        unread = psum.tile([M_TILE, V], F32, name="unread", tag="bank7")
+        nc.tensor.matmul_mx(
+            unread[:],
+            lhsT=ew[:, :M_TILE].bitcast(FP8X4),
+            lhsT_scale=spread[:, S : S + M_TILE],
+            rhs=xw[:].bitcast(FP8X4),
+            rhs_scale=spread[:, :S],
+            start=True,
+            stop=True,
+        )
         for i in range(2):
             bank(i, 0)
             long_term(i, 0, True)
@@ -193,13 +204,8 @@ def tile_picked_zsess_sigmoid_p_kernel(
             piece(i, 1)
 
         late = [cast(nc.vector.tensor_copy, h_late[:, :, span(i, M_TILE)], "h_late_bf%d" % i) for i in range(2)]
-        q = quantize(late[0], "h_late0")
-        h_codes.append((q[0][:], q[1][:]))
-        for b in range(2):
-            piece(2, b)
-        xw3 = gather(xw_table[:].bitcast(U32), offs_sb[:, columns(3 * M_TILE, M_TILE)], U32, "xw3", tag="h_raw2")
-        x_codes.append(xw3[:])
-        q = quantize(late[1], "h_late1")
-        h_codes.append((q[0][:], q[1][:]))
-        for b in range(2):
-            piece(3, b)
+        for i in range(2):
+            q = quantize(late[i], "h_late%d" % i)
+            h_codes.append((q[0][:], q[1][:]))
+            for b in range(2):
+                piece(2 + i, b)

@@ -126,7 +126,7 @@ def tile_picked_zsess_sigmoid_p_kernel(
         xs_table = zeroed(T, "xs_table")
         es_table = zeroed(W, "es_table")
         fs_table = zeroed(W, "fs_table")
-        plane = tile_at([P, S + 2 * V], U8, "plane")
+        plane = zeroed(S + 2 * V, "plane")
         xw_table = tile_at([P, T], I32, "xw_table")
         x_rows = x_words[0].rearrange("p n t -> p (n t)").bitcast(I32)
         x_split = T // 2
@@ -146,8 +146,7 @@ def tile_picked_zsess_sigmoid_p_kernel(
         nc.vector.tensor_copy(spread[:, :S], xs_table[:].indirect(offs_sb[:]))
         nc.vector.tensor_copy(spread[:, S : S + V], es_table[:].indirect(cand_sb[:]))
         nc.vector.tensor_copy(spread[:, S + V :], fs_table[:].indirect(cand_sb[:]))
-        nc.vector.tensor_copy(plane[:].bitcast(I32), spread[:].bitcast(I32))
-        for r in range(1, ROWS):
+        for r in range(ROWS):
             move_rows(plane, spread, r)
         xs, es, fs = plane[:, :S], plane[:, S : S + V], plane[:, S + V :]
         h_late = load_h(2, 2)

@@ -202,9 +202,30 @@ def tile_picked_zsess_sigmoid_p_kernel(
         for i in range(2):
             piece(i, 1)
 
-        late = [cast(nc.vector.tensor_copy, h_late[:, :, span(i, M_TILE)], "h_late_bf%d" % i) for i in range(2)]
-        for i in range(2):
-            q = quantize(late[i], "h_late%d" % i)
+        for b in range(2):
+            bank(2, b)
+            long_term(2, b, True)
+
+        third = cast(nc.vector.tensor_copy, h_late[:, :, :M_TILE], "h_late_bf0")
+        fourth = tile_at([P, M_TILE, PACK], BF16, "h_late_bf1")
+
+        def cast_half(half):
+            users = span(half, M_TILE // 2)
+            nc.vector.tensor_copy(
+                fourth[:, users, :].rearrange("p (c i) j -> p c j i", i=RUN),
+                h_late[:, :, M_TILE + users.start : M_TILE + users.stop].rearrange("p j (c i) -> p c j i", i=RUN),
+            )
+
+        def close(i, grouped):
+            q = quantize(grouped, "h_late%d" % i)
             h_codes.append((q[0][:], q[1][:]))
-            for b in range(2):
-                piece(2 + i, b)
+
+        cast_half(0)
+        close(2, third)
+        for b in range(2):
+            session(2, b, False)
+            leave(2, b)
+        cast_half(1)
+        close(3, fourth)
+        for b in range(2):
+            piece(3, b)

@@ -13,8 +13,6 @@ U16 = mybir.dt.uint16
 U8 = mybir.dt.uint8
 FP8X4 = mybir.dt.float8_e4m3fn_x4
 SIGMOID = mybir.ActivationFunctionType.Sigmoid
-MULT = mybir.AluOpType.mult
-ADD = mybir.AluOpType.add
 
 P = 128
 PACK = 4
@@ -26,7 +24,6 @@ RUN = 4
 M_TILE = 128
 N_HALF = 256
 ALIGN = 64
-X_ROW = 8
 
 
 def tile_picked_zsess_sigmoid_p_kernel(
@@ -35,76 +32,59 @@ def tile_picked_zsess_sigmoid_p_kernel(
     nc = tc.nc
     with ExitStack() as ctx:
         lists = ctx.enter_context(tc.tile_pool(name="lists", bufs=1))
-        tables = ctx.enter_context(tc.tile_pool(name="tables", bufs=1))
-        keep = ctx.enter_context(tc.tile_pool(name="keep", bufs=1))
+        sbuf = ctx.enter_context(tc.tile_pool(name="sbuf", bufs=1))
         placed = ctx.enter_context(tc.tile_pool(name="placed", bufs=1))
         psum = ctx.enter_context(tc.psum_pool(name="psum", bufs=1))
 
         offs_sb = lists.tile([P, S // LIST_COLUMN], U16, name="offs_sb")
         cand_sb = lists.tile([P, V // LIST_COLUMN], U16, name="cand_sb")
 
-        def tile_at(shape, dtype, name, at=None, tag=None):
-            if at is None:
-                return tables.tile(shape, dtype, name=name, tag=tag or name, align_bytes=ALIGN)
-            return placed.tile(shape, dtype, name=name, offset=at, align_bytes=ALIGN)
+        def tile(shape, dtype, name, tag=None, at=None):
+            if at is not None:
+                return placed.tile(shape, dtype, name=name, offset=at, align_bytes=ALIGN)
+            return sbuf.tile(shape, dtype, name=name, tag=tag or name, align_bytes=ALIGN)
 
-        def load_words(words, columns, name, at=None):
-            table = tile_at([P, columns], I32, name, at)
-            nc.sync.dma_start(table[:], words[0].rearrange("p n t -> p (n t)").bitcast(I32))
+        def span(i, n, count=1):
+            return slice(i * n, (i + count) * n)
+
+        def entries(part):
+            return slice(part.start // LIST_COLUMN, part.stop // LIST_COLUMN)
+
+        def load_words(table, words, part):
+            rows = words[0].rearrange("p n t -> p (n t)").bitcast(I32)
+            nc.sync.dma_start(table[:, part], rows[:, part])
+
+        def zeroed(columns, name, at=None):
+            table = tile([P, columns], U8, name, at=at)
+            nc.vector.memset(table[:].bitcast(I32), 0)
             return table
 
-        def zeroed(columns, name, engine=nc.vector, at=None):
-            table = tile_at([P, columns], U8, name, at)
-            engine.memset(table[:].bitcast(I32), 0)
-            return table
+        def load_spread(table, scales):
+            nc.sync.dma_start(table[0:P:SPREAD, :].bitcast(I32), scales[0].bitcast(I32))
 
-        def load_spread(table, scales, first=0):
-            nc.sync.dma_start(table[first:P:SPREAD, :].bitcast(I32), scales[0].bitcast(I32))
+        def move_rows(plane, spread, r):
+            nc.sync.dma_start(plane[r:P:QUADRANT].bitcast(I32), spread[SPREAD * r : P : QUADRANT].bitcast(I32))
 
-        def load_scale_rows(table, scales, first_row, r):
-            nc.sync.dma_start(
-                table[first_row + r : P : QUADRANT, :].bitcast(I32),
-                scales[0, r : K // 32 : ROWS, :].bitcast(I32),
-            )
-
-        def move_rows(plane, spread, r, first=0, queue=nc.sync):
-            queue.dma_start(
-                plane[r:P:QUADRANT].bitcast(I32),
-                spread[first + SPREAD * r : P : QUADRANT].bitcast(I32),
-            )
-
-        def load_h(first, count, at=None):
-            name = "h_raw%d" % first
-            raw = tile_at([P, PACK, count * M_TILE], F32, name, at)
-            users = slice(first * M_TILE, (first + count) * M_TILE)
+        def load_h(users, name, at=None):
+            raw = tile([P, PACK, users.stop - users.start], F32, name, at=at)
             nc.sync.dma_start(raw[:], hT[:, users].rearrange("(p j) t -> p j t", j=PACK))
             return raw
 
-        def gather(table, offsets, dtype, name, tag=None):
-            picked = tables.tile([P, LIST_COLUMN * offsets.shape[1]], dtype, name=name, tag=tag or name, align_bytes=ALIGN)
-            nc.vector.tensor_copy(picked[:], table.indirect(offsets))
-            return picked
+        def gather(picked, table, offsets):
+            nc.vector.tensor_copy(picked, table.indirect(offsets))
 
-        def cast(copy, raw, name, tag=None):
-            grouped = tables.tile([P, raw.shape[2], PACK], BF16, name=name, tag=tag or name, align_bytes=ALIGN)
+        def cast(copy, grouped, raw):
             copy(
-                grouped[:].rearrange("p (c i) j -> p c j i", i=RUN),
+                grouped.rearrange("p (c i) j -> p c j i", i=RUN),
                 raw.rearrange("p j (c i) -> p c j i", i=RUN),
             )
-            return grouped
 
         def quantize(grouped, name, tag=None):
             users = grouped.shape[1]
-            codes = tables.tile([P, users], U32, name=name + "_codes", tag=tag or name, align_bytes=ALIGN)
-            scales = keep.tile([P, users], U8, name=name + "_scales", align_bytes=ALIGN)
-            nc.vector.quantize_mx(codes[:].bitcast(FP8X4), scales[:], grouped[:].rearrange("p t j -> p (t j)"))
+            codes = tile([P, users], U32, name + "_codes", tag)
+            scales = tile([P, users], U8, name + "_scales")
+            nc.vector.quantize_mx(codes[:].bitcast(FP8X4), scales[:], grouped.rearrange("p t j -> p (t j)"))
             return codes, scales
-
-        def columns(first, count):
-            return slice(first // LIST_COLUMN, (first + count) // LIST_COLUMN)
-
-        def span(i, n):
-            return slice(i * n, (i + 1) * n)
 
         def product(acc, lhs, lhs_scale, rhs, rhs_scale, first):
             nc.tensor.matmul_mx(
@@ -117,115 +97,104 @@ def tile_picked_zsess_sigmoid_p_kernel(
                 stop=not first,
             )
 
-        def emit(acc, i, items, name, tag=None, queue=nc.sync):
-            result = tables.tile([M_TILE, items.stop - items.start], F32, name=name, tag=tag or name, align_bytes=ALIGN)
+        def emit(acc, i, items, queue=nc.sync):
+            result = tile([M_TILE, items.stop - items.start], F32, "result%d_%d" % (i, items.start))
             nc.scalar.activation(result[:], acc, SIGMOID)
-            queue.dma_start(out[i * M_TILE : (i + 1) * M_TILE, items], result[:])
-
+            queue.dma_start(out[span(i, M_TILE), items], result[:])
 
         xs_table = zeroed(T, "xs_table")
         es_table = zeroed(W, "es_table")
         fs_table = zeroed(W, "fs_table")
         plane = zeroed(S + 2 * V, "plane")
-        xw_table = tile_at([P, T], I32, "xw_table")
-        x_rows = x_words[0].rearrange("p n t -> p (n t)").bitcast(I32)
-        x_split = T // 2
+        xw_table = tile([P, T], I32, "xw_table")
+        ew_table = tile([P, W], I32, "ew_table")
+        fw_table = tile([P, W], I32, "fw_table")
+        h_early = tile([P, PACK, 2 * M_TILE], F32, "h_early")
+        early_rows = hT[:, span(0, M_TILE, 2)].rearrange("(p j) t -> p j t", j=PACK)
 
-        nc.sync.dma_start(xw_table[:, :x_split], x_rows[:, :x_split])
+        nc.sync.dma_start(h_early[:, :2, :], early_rows[:, :2, :])
         nc.sync.dma_start(offs_sb[:], offs)
         load_spread(xs_table, x_scales)
-        nc.sync.dma_start(xw_table[:, x_split:], x_rows[:, x_split:])
         nc.sync.dma_start(cand_sb[:], cand)
+        nc.sync.dma_start(h_early[:, 2:, :], early_rows[:, 2:, :])
         load_spread(es_table, e_scales)
-        h_early = load_h(0, 2)
         load_spread(fs_table, f_scales)
-        ew_table = load_words(e_words, W, "ew_table")
-        fw_table = load_words(f_words, W, "fw_table")
+        load_words(fw_table, f_words, slice(0, W))
+        load_words(ew_table, e_words, slice(0, W))
 
-        spread = tile_at([P, S + 2 * V], U8, "spread")
-        nc.vector.tensor_copy(spread[:, :S], xs_table[:].indirect(offs_sb[:]))
-        nc.vector.tensor_copy(spread[:, S : S + V], es_table[:].indirect(cand_sb[:]))
-        nc.vector.tensor_copy(spread[:, S + V :], fs_table[:].indirect(cand_sb[:]))
+        spread = tile([P, S + 2 * V], U8, "spread")
+        gather(spread[:, :S], xs_table[:], offs_sb[:])
+        gather(spread[:, S : S + V], es_table[:], cand_sb[:])
+        gather(spread[:, S + V :], fs_table[:], cand_sb[:])
         for r in range(ROWS):
             move_rows(plane, spread, r)
         xs, es, fs = plane[:, :S], plane[:, S : S + V], plane[:, S + V :]
-        h_late = load_h(2, 2)
+        load_words(xw_table, x_words, slice(0, T))
+        h_late = {i: load_h(span(i, M_TILE), "h_late%d" % i) for i in (2, 3)}
 
-        early_bf = cast(nc.scalar.copy, h_early[:], "h_early_bf")
-        xw = gather(xw_table[:].bitcast(U32), offs_sb[:], U32, "xw", tag="h_raw0")
-        x_codes = [xw[:, span(i, M_TILE)] for i in range(4)]
-        early = quantize(early_bf, "h_early")
-        h_codes = [(early[0][:, span(i, M_TILE)], early[1][:, span(i, M_TILE)]) for i in range(2)]
+        fw = tile([P, V], U32, "fw")
+        gather(fw[:], fw_table[:].bitcast(U32), cand_sb[:])
 
+        pair_bf = tile([P, 2 * M_TILE, PACK], BF16, "pair_bf")
+        cast(nc.scalar.copy, pair_bf[:], h_early[:])
+        pair = quantize(pair_bf[:], "pair")
+        h_codes = [(pair[0][:, span(i, M_TILE)], pair[1][:, span(i, M_TILE)]) for i in range(2)]
+
+        halves = [span(b, N_HALF) for b in range(2)]
+        pieces = [halves, halves, halves, halves]
         acc = {}
-        fw = []
-        ew = tile_at([P, V], U32, "ew")
 
-        def long_term(i, b, first):
-            product(acc[i, b][:], x_codes[i], xs[:, span(i, M_TILE)], ew[:, span(b, N_HALF)], es[:, span(b, N_HALF)], first)
+        def session(i, items, first):
+            product(acc[i, items.start][:], h_codes[i][0], h_codes[i][1], fw[:, items], fs[:, items], first)
 
-        def session(i, b, first):
-            product(acc[i, b][:], h_codes[i][0], h_codes[i][1], fw[b][:], fs[:, span(b, N_HALF)], first)
+        def bank(i, items):
+            acc[i, items.start] = psum.tile([M_TILE, items.stop - items.start], F32, name="acc%d_%d" % (i, items.start))
 
-        def leave(i, b):
-            emit(acc[i, b][:], i, span(b, N_HALF), "result%d_%d" % (i, b))
-
-        def bank(i, b):
-            acc[i, b] = psum.tile([M_TILE, N_HALF], F32, name="acc%d_%d" % (i, b), tag="bank%d" % (2 * i + b))
-
-        def piece(i, b):
-            bank(i, b)
-            session(i, b, True)
-            long_term(i, b, False)
-            leave(i, b)
-
-        for b in range(2):
-            nc.vector.tensor_copy(ew[:, span(b, N_HALF)], ew_table[:].bitcast(U32).indirect(cand_sb[:, columns(b * N_HALF, N_HALF)]))
-        unread = psum.tile([M_TILE, V], F32, name="unread", tag="bank7")
-        nc.tensor.matmul_mx(
-            unread[:],
-            lhsT=ew[:, :M_TILE].bitcast(FP8X4),
-            lhsT_scale=spread[:, S : S + M_TILE],
-            rhs=xw[:].bitcast(FP8X4),
-            rhs_scale=spread[:, :S],
-            start=True,
-            stop=True,
-        )
         for i in range(2):
-            bank(i, 0)
-            long_term(i, 0, True)
-        fw.append(gather(fw_table[:].bitcast(U32), cand_sb[:, columns(0, N_HALF)], U32, "fw0"))
+            for items in pieces[i]:
+                bank(i, items)
+                session(i, items, True)
+
+        ew = tile([P, V], U32, "ew", "pair_bf")
+        for items in halves:
+            gather(ew[:, items], ew_table[:].bitcast(U32), cand_sb[:, entries(items)])
+
+        xw = {}
+
+        def long_term(i, items, first):
+            product(acc[i, items.start][:], xw[i][:], xs[:, span(i, M_TILE)], ew[:, items], es[:, items], first)
+
+        def pick_users(i, tag=None):
+            xw[i] = tile([P, M_TILE], U32, "xw%d" % i, tag)
+            gather(xw[i][:], xw_table[:].bitcast(U32), offs_sb[:, entries(span(i, M_TILE))])
+
+        def open_late(i):
+            for items in pieces[i]:
+                bank(i, items)
+                long_term(i, items, True)
+
+        def round_late(i):
+            rounded = tile([P, M_TILE, PACK], BF16, "late_bf%d" % i)
+            cast(nc.vector.tensor_copy, rounded[:], h_late[i][:])
+            return rounded
+
+        def close_late(i, rounded):
+            codes, scales = quantize(rounded[:], "late%d" % i)
+            h_codes.append((codes[:], scales[:]))
+            for items in pieces[i]:
+                session(i, items, False)
+                emit(acc[i, items.start][:], i, items)
+
         for i in range(2):
-            session(i, 0, False)
-            leave(i, 0)
-        fw.append(gather(fw_table[:].bitcast(U32), cand_sb[:, columns(N_HALF, N_HALF)], U32, "fw1"))
-        for i in range(2):
-            piece(i, 1)
+            pick_users(i)
+            for items in pieces[i]:
+                long_term(i, items, False)
+                emit(acc[i, items.start][:], i, items)
 
-        for b in range(2):
-            bank(2, b)
-            long_term(2, b, True)
-
-        third = cast(nc.vector.tensor_copy, h_late[:, :, :M_TILE], "h_late_bf0")
-        fourth = tile_at([P, M_TILE, PACK], BF16, "h_late_bf1")
-
-        def cast_half(half):
-            users = span(half, M_TILE // 2)
-            nc.vector.tensor_copy(
-                fourth[:, users, :].rearrange("p (c i) j -> p c j i", i=RUN),
-                h_late[:, :, M_TILE + users.start : M_TILE + users.stop].rearrange("p j (c i) -> p c j i", i=RUN),
-            )
-
-        def close(i, grouped):
-            q = quantize(grouped, "h_late%d" % i)
-            h_codes.append((q[0][:], q[1][:]))
-
-        cast_half(0)
-        close(2, third)
-        for b in range(2):
-            session(2, b, False)
-            leave(2, b)
-        cast_half(1)
-        close(3, fourth)
-        for b in range(2):
-            piece(3, b)
+        pick_users(2)
+        open_late(2)
+        rounded = round_late(2)
+        pick_users(3, "xw0")
+        open_late(3)
+        close_late(2, rounded)
+        close_late(3, round_late(3))

@@ -18,7 +18,8 @@ P = 128
 PACK = 4
 QUADRANT = 32
 ROWS = 4
-SPREAD = 8
+SPREAD = 7
+FIRST = 11
 LIST_COLUMN = 16
 RUN = 4
 M_TILE = 128
@@ -60,10 +61,10 @@ def tile_picked_zsess_sigmoid_p_kernel(
             return table
 
         def load_spread(table, scales):
-            nc.sync.dma_start(table[0:P:SPREAD, :].bitcast(I32), scales[0].bitcast(I32))
+            nc.sync.dma_start(table[FIRST : FIRST + SPREAD * (K // 32) : SPREAD, :].bitcast(I32), scales[0].bitcast(I32))
 
         def move_rows(plane, spread, r):
-            nc.sync.dma_start(plane[r:P:QUADRANT].bitcast(I32), spread[SPREAD * r : P : QUADRANT].bitcast(I32))
+            nc.sync.dma_start(plane[r:P:QUADRANT].bitcast(I32), spread[FIRST + SPREAD * r : FIRST + SPREAD * (K // 32) : SPREAD * ROWS].bitcast(I32))
 
         def load_h(users, name, at=None):
             raw = tile([P, PACK, users.stop - users.start], F32, name, at=at)
@@ -197,4 +198,17 @@ def tile_picked_zsess_sigmoid_p_kernel(
         pick_users(3, "xw0")
         open_late(3)
         close_late(2, rounded)
-        close_late(3, round_late(3))
+        last_bf = tile([P, M_TILE, PACK], BF16, "late_bf3")
+        last_codes = tile([P, M_TILE], U32, "late3_codes")
+        last_scales = tile([P, M_TILE], U8, "late3_scales")
+        parts = [span(a, M_TILE // 2) for a in range(2)]
+        for part in parts:
+            cast(nc.vector.tensor_copy, last_bf[:, part, :], h_late[3][:, :, part])
+        for part in parts:
+            nc.vector.quantize_mx(
+                last_codes[:, part].bitcast(FP8X4), last_scales[:, part], last_bf[:, part, :].rearrange("p t j -> p (t j)")
+            )
+        h_codes.append((last_codes[:], last_scales[:]))
+        for items in pieces[3]:
+            session(3, items, False)
+            emit(acc[3, items.start][:], 3, items)

@@ -113,11 +113,11 @@ def tile_picked_zsess_sigmoid_p_kernel(
         h_early = tile([P, PACK, 2 * M_TILE], F32, "h_early")
         early_rows = hT[:, span(0, M_TILE, 2)].rearrange("(p j) t -> p j t", j=PACK)
 
-        nc.sync.dma_start(h_early[:, :2, :], early_rows[:, :2, :])
+        nc.sync.dma_start(h_early[:, :1, :], early_rows[:, :1, :])
         nc.sync.dma_start(offs_sb[:], offs)
         load_spread(xs_table, x_scales)
         nc.sync.dma_start(cand_sb[:], cand)
-        nc.sync.dma_start(h_early[:, 2:, :], early_rows[:, 2:, :])
+        nc.sync.dma_start(h_early[:, 1:, :], early_rows[:, 1:, :])
         load_spread(es_table, e_scales)
         load_spread(fs_table, f_scales)
         load_words(fw_table, f_words, slice(0, W))

@@ -98,10 +98,14 @@ def tile_picked_zsess_sigmoid_p_kernel(
                 stop=not first,
             )
 
-        def emit(acc, i, items, queue=nc.sync):
-            result = tile([M_TILE, items.stop - items.start], F32, "result%d_%d" % (i, items.start))
+        def emit(acc, i, items, queue=nc.sync, at=None):
+            result = tile([M_TILE, items.stop - items.start], F32, "result%d_%d" % (i, items.start), at=at)
             nc.scalar.activation(result[:], acc, SIGMOID)
             queue.dma_start(out[span(i, M_TILE), items], result[:])
+
+        unread = tile([P, 2], F32, "unread")
+        nc.gpsimd.memset(unread[:, :1], 0.0)
+        nc.scalar.activation(unread[:, 1:], unread[:, :1], SIGMOID)
 
         xs_table = zeroed(T, "xs_table")
         es_table = zeroed(W, "es_table")
@@ -110,14 +114,15 @@ def tile_picked_zsess_sigmoid_p_kernel(
         xw_table = tile([P, T], I32, "xw_table")
         ew_table = tile([P, W], I32, "ew_table")
         fw_table = tile([P, W], I32, "fw_table")
-        h_early = tile([P, PACK, 2 * M_TILE], F32, "h_early")
-        early_rows = hT[:, span(0, M_TILE, 2)].rearrange("(p j) t -> p j t", j=PACK)
+        h_raw = tile([P, PACK, 3 * M_TILE], F32, "h_raw", at=0)
+        h_rows = hT[:, span(0, M_TILE, 3)].rearrange("(p j) t -> p j t", j=PACK)
+        early = span(0, M_TILE, 2)
 
-        nc.sync.dma_start(h_early[:, :1, :], early_rows[:, :1, :])
+        nc.sync.dma_start(h_raw[:, 0, :], h_rows[:, 0, :])
         nc.sync.dma_start(offs_sb[:], offs)
         load_spread(xs_table, x_scales)
         nc.sync.dma_start(cand_sb[:], cand)
-        nc.sync.dma_start(h_early[:, 1:, :], early_rows[:, 1:, :])
+        nc.sync.dma_start(h_raw[:, 1:, early], h_rows[:, 1:, early])
         load_spread(es_table, e_scales)
         load_spread(fs_table, f_scales)
         load_words(fw_table, f_words, slice(0, W))
@@ -131,13 +136,14 @@ def tile_picked_zsess_sigmoid_p_kernel(
             move_rows(plane, spread, r)
         xs, es, fs = plane[:, :S], plane[:, S : S + V], plane[:, S + V :]
         load_words(xw_table, x_words, slice(0, T))
-        h_late = {i: load_h(span(i, M_TILE), "h_late%d" % i) for i in (2, 3)}
+        nc.sync.dma_start(h_raw[:, 1:, span(2, M_TILE)], h_rows[:, 1:, span(2, M_TILE)])
+        h_late = {2: h_raw[:, :, span(2, M_TILE)], 3: load_h(span(3, M_TILE), "h_late3")}
 
         fw = tile([P, V], U32, "fw")
         gather(fw[:], fw_table[:].bitcast(U32), cand_sb[:])
 
         pair_bf = tile([P, 2 * M_TILE, PACK], BF16, "pair_bf")
-        cast(nc.scalar.copy, pair_bf[:], h_early[:])
+        cast(nc.scalar.copy, pair_bf[:], h_raw[:, :, early])
         pair = quantize(pair_bf[:], "pair")
         h_codes = [(pair[0][:, span(i, M_TILE)], pair[1][:, span(i, M_TILE)]) for i in range(2)]
 
@@ -170,35 +176,37 @@ def tile_picked_zsess_sigmoid_p_kernel(
             gather(xw[i][:], xw_table[:].bitcast(U32), offs_sb[:, entries(span(i, M_TILE))])
 
         def open_late(i):
-            for items in pieces[i]:
-                bank(i, items)
-                long_term(i, items, True)
+            bank(i, pieces[i][0])
+            long_term(i, pieces[i][0], True)
 
         def round_late(i):
             rounded = tile([P, M_TILE, PACK], BF16, "late_bf%d" % i)
-            cast(nc.vector.tensor_copy, rounded[:], h_late[i][:])
+            cast(nc.scalar.copy, rounded[:], h_late[i])
             return rounded
 
         def close_late(i, rounded):
             codes, scales = quantize(rounded[:], "late%d" % i)
             h_codes.append((codes[:], scales[:]))
-            for items in pieces[i]:
-                session(i, items, False)
-                emit(acc[i, items.start][:], i, items)
+            first, second = pieces[i]
+            session(i, first, False)
+            emit(acc[i, first.start][:], i, first)
+            bank(i, second)
+            session(i, second, True)
+            long_term(i, second, False)
+            emit(acc[i, second.start][:], i, second)
 
+        rounded = round_late(2)
         for i in range(2):
             pick_users(i)
             for items in pieces[i]:
                 long_term(i, items, False)
-                emit(acc[i, items.start][:], i, items)
+                emit(acc[i, items.start][:], i, items, at=0 if (i, items.start) == (0, 0) else None)
 
         pick_users(2)
         open_late(2)
-        rounded = round_late(2)
-        pick_users(3, "xw0")
-        open_late(3)
+        pick_users(3)
         close_late(2, rounded)
-        last_bf = tile([P, M_TILE, PACK], BF16, "late_bf3")
+        last_bf = tile([P, M_TILE, PACK], BF16, "late_bf3", at=4 * N_HALF)
         last_codes = tile([P, M_TILE], U32, "late3_codes")
         last_scales = tile([P, M_TILE], U8, "late3_scales")
         parts = [span(a, M_TILE // 2) for a in range(2)]
@@ -210,5 +218,7 @@ def tile_picked_zsess_sigmoid_p_kernel(
             )
         h_codes.append((last_codes[:], last_scales[:]))
         for items in pieces[3]:
-            session(3, items, False)
+            bank(3, items)
+            session(3, items, True)
+            long_term(3, items, False)
             emit(acc[3, items.start][:], 3, items)

from contextlib import ExitStack

import concourse.mybir as mybir

K, T, S, V, W = 512, 1024, 512, 512, 2048
FLOPS = 2 * 2 * K * S * V

F32 = mybir.dt.float32
BF16 = mybir.dt.bfloat16
I32 = mybir.dt.int32
U32 = mybir.dt.uint32
U16 = mybir.dt.uint16
U8 = mybir.dt.uint8
FP8X4 = mybir.dt.float8_e4m3fn_x4
SIGMOID = mybir.ActivationFunctionType.Sigmoid

P = 128
PACK = 4
QUADRANT = 32
ROWS = 4
SPREAD = 7
FIRST = 11
LIST_COLUMN = 16
RUN = 4
M_TILE = 128
N_HALF = 256
ALIGN = 64


def tile_picked_zsess_sigmoid_p_kernel(
    tc, x_words, x_scales, e_words, e_scales, f_words, f_scales, hT, offs, cand, out
):
    nc = tc.nc
    with ExitStack() as ctx:
        lists = ctx.enter_context(tc.tile_pool(name="lists", bufs=1))
        sbuf = ctx.enter_context(tc.tile_pool(name="sbuf", bufs=1))
        placed = ctx.enter_context(tc.tile_pool(name="placed", bufs=1))
        psum = ctx.enter_context(tc.psum_pool(name="psum", bufs=1))

        offs_sb = lists.tile([P, S // LIST_COLUMN], U16, name="offs_sb")
        cand_sb = lists.tile([P, V // LIST_COLUMN], U16, name="cand_sb")

        def tile(shape, dtype, name, tag=None, at=None):
            if at is not None:
                return placed.tile(shape, dtype, name=name, offset=at, align_bytes=ALIGN)
            return sbuf.tile(shape, dtype, name=name, tag=tag or name, align_bytes=ALIGN)

        def span(i, n, count=1):
            return slice(i * n, (i + count) * n)

        def entries(part):
            return slice(part.start // LIST_COLUMN, part.stop // LIST_COLUMN)

        def load_words(table, words, part):
            rows = words[0].rearrange("p n t -> p (n t)").bitcast(I32)
            nc.sync.dma_start(table[:, part], rows[:, part])

        def zeroed(columns, name, at=None):
            table = tile([P, columns], U8, name, at=at)
            nc.vector.memset(table[:].bitcast(I32), 0)
            return table

        def load_spread(table, scales):
            nc.sync.dma_start(table[FIRST : FIRST + SPREAD * (K // 32) : SPREAD, :].bitcast(I32), scales[0].bitcast(I32))

        def move_rows(plane, spread, r):
            nc.sync.dma_start(plane[r:P:QUADRANT].bitcast(I32), spread[FIRST + SPREAD * r : FIRST + SPREAD * (K // 32) : SPREAD * ROWS].bitcast(I32))

        def load_h(users, name, at=None):
            raw = tile([P, PACK, users.stop - users.start], F32, name, at=at)
            nc.sync.dma_start(raw[:], hT[:, users].rearrange("(p j) t -> p j t", j=PACK))
            return raw

        def gather(picked, table, offsets):
            nc.vector.tensor_copy(picked, table.indirect(offsets))

        def cast(copy, grouped, raw):
            copy(
                grouped.rearrange("p (c i) j -> p c j i", i=RUN),
                raw.rearrange("p j (c i) -> p c j i", i=RUN),
            )

        def quantize(grouped, name, tag=None):
            users = grouped.shape[1]
            codes = tile([P, users], U32, name + "_codes", tag)
            scales = tile([P, users], U8, name + "_scales")
            nc.vector.quantize_mx(codes[:].bitcast(FP8X4), scales[:], grouped.rearrange("p t j -> p (t j)"))
            return codes, scales

        def product(acc, lhs, lhs_scale, rhs, rhs_scale, first):
            nc.tensor.matmul_mx(
                acc,
                lhsT=lhs.bitcast(FP8X4),
                lhsT_scale=lhs_scale,
                rhs=rhs.bitcast(FP8X4),
                rhs_scale=rhs_scale,
                start=first,
                stop=not first,
            )

        def emit(acc, i, items, queue=nc.sync, at=None):
            result = tile([M_TILE, items.stop - items.start], F32, "result%d_%d" % (i, items.start), at=at)
            nc.scalar.activation(result[:], acc, SIGMOID)
            queue.dma_start(out[span(i, M_TILE), items], result[:])

        unread = tile([P, 2], F32, "unread")
        nc.gpsimd.memset(unread[:, :1], 0.0)
        nc.scalar.activation(unread[:, 1:], unread[:, :1], SIGMOID)

        xs_table = zeroed(T, "xs_table")
        es_table = zeroed(W, "es_table")
        fs_table = zeroed(W, "fs_table")
        plane = zeroed(S + 2 * V, "plane")
        xw_table = tile([P, T], I32, "xw_table")
        ew_table = tile([P, W], I32, "ew_table")
        fw_table = tile([P, W], I32, "fw_table")
        h_raw = tile([P, PACK, 3 * M_TILE], F32, "h_raw", at=0)
        h_rows = hT[:, span(0, M_TILE, 3)].rearrange("(p j) t -> p j t", j=PACK)
        early = span(0, M_TILE, 2)

        nc.sync.dma_start(h_raw[:, 0, :], h_rows[:, 0, :])
        nc.sync.dma_start(offs_sb[:], offs)
        load_spread(xs_table, x_scales)
        nc.sync.dma_start(cand_sb[:], cand)
        nc.sync.dma_start(h_raw[:, 1:, early], h_rows[:, 1:, early])
        load_spread(es_table, e_scales)
        load_spread(fs_table, f_scales)
        load_words(fw_table, f_words, slice(0, W))
        load_words(ew_table, e_words, slice(0, W))

        spread = tile([P, S + 2 * V], U8, "spread")
        gather(spread[:, :S], xs_table[:], offs_sb[:])
        gather(spread[:, S : S + V], es_table[:], cand_sb[:])
        gather(spread[:, S + V :], fs_table[:], cand_sb[:])
        for r in range(ROWS):
            move_rows(plane, spread, r)
        xs, es, fs = plane[:, :S], plane[:, S : S + V], plane[:, S + V :]
        load_words(xw_table, x_words, slice(0, T))
        nc.sync.dma_start(h_raw[:, 1:, span(2, M_TILE)], h_rows[:, 1:, span(2, M_TILE)])
        h_late = {2: h_raw[:, :, span(2, M_TILE)], 3: load_h(span(3, M_TILE), "h_late3")}

        fw = tile([P, V], U32, "fw")
        gather(fw[:], fw_table[:].bitcast(U32), cand_sb[:])

        pair_bf = tile([P, 2 * M_TILE, PACK], BF16, "pair_bf")
        cast(nc.scalar.copy, pair_bf[:], h_raw[:, :, early])
        pair = quantize(pair_bf[:], "pair")
        h_codes = [(pair[0][:, span(i, M_TILE)], pair[1][:, span(i, M_TILE)]) for i in range(2)]

        halves = [span(b, N_HALF) for b in range(2)]
        pieces = [halves, halves, halves, halves]
        acc = {}

        def session(i, items, first):
            product(acc[i, items.start][:], h_codes[i][0], h_codes[i][1], fw[:, items], fs[:, items], first)

        def bank(i, items):
            acc[i, items.start] = psum.tile([M_TILE, items.stop - items.start], F32, name="acc%d_%d" % (i, items.start))

        for i in range(2):
            for items in pieces[i]:
                bank(i, items)
                session(i, items, True)

        ew = tile([P, V], U32, "ew", "pair_bf")
        for items in halves:
            gather(ew[:, items], ew_table[:].bitcast(U32), cand_sb[:, entries(items)])

        xw = {}

        def long_term(i, items, first):
            product(acc[i, items.start][:], xw[i][:], xs[:, span(i, M_TILE)], ew[:, items], es[:, items], first)

        def pick_users(i, tag=None):
            xw[i] = tile([P, M_TILE], U32, "xw%d" % i, tag)
            gather(xw[i][:], xw_table[:].bitcast(U32), offs_sb[:, entries(span(i, M_TILE))])

        def open_late(i):
            bank(i, pieces[i][0])
            long_term(i, pieces[i][0], True)

        def round_late(i):
            rounded = tile([P, M_TILE, PACK], BF16, "late_bf%d" % i)
            cast(nc.scalar.copy, rounded[:], h_late[i])
            return rounded

        def close_late(i, rounded):
            codes, scales = quantize(rounded[:], "late%d" % i)
            h_codes.append((codes[:], scales[:]))
            first, second = pieces[i]
            session(i, first, False)
            emit(acc[i, first.start][:], i, first)
            bank(i, second)
            session(i, second, True)
            long_term(i, second, False)
            emit(acc[i, second.start][:], i, second)

        rounded = round_late(2)
        for i in range(2):
            pick_users(i)
            for items in pieces[i]:
                long_term(i, items, False)
                emit(acc[i, items.start][:], i, items, at=0 if (i, items.start) == (0, 0) else None)

        pick_users(2)
        open_late(2)
        pick_users(3)
        close_late(2, rounded)
        last_bf = tile([P, M_TILE, PACK], BF16, "late_bf3", at=4 * N_HALF)
        last_codes = tile([P, M_TILE], U32, "late3_codes")
        last_scales = tile([P, M_TILE], U8, "late3_scales")
        parts = [span(a, M_TILE // 2) for a in range(2)]
        for part in parts:
            cast(nc.vector.tensor_copy, last_bf[:, part, :], h_late[3][:, :, part])
        for part in parts:
            nc.vector.quantize_mx(
                last_codes[:, part].bitcast(FP8X4), last_scales[:, part], last_bf[:, part, :].rearrange("p t j -> p (t j)")
            )
        h_codes.append((last_codes[:], last_scales[:]))
        for items in pieces[3]:
            bank(3, items)
            session(3, items, True)
            long_term(3, items, False)
            emit(acc[3, items.start][:], 3, items)
